import numpy as np
import ml_dtypes


def mxq(x, axis, fmt="e4m3"):
    dtype, down = {"e4m3": (ml_dtypes.float8_e4m3fn, 7), "e5m2": (ml_dtypes.float8_e5m2, 14)}[fmt]
    v = np.moveaxis(np.asarray(x, np.float32).astype(ml_dtypes.bfloat16).astype(np.float64), axis, -1)
    blocks = v.reshape(v.shape[:-1] + (-1, 32))
    amax = np.abs(blocks).max(-1, keepdims=True)
    byte = np.maximum(np.where(amax > 0, np.frexp(amax)[1] - 1 + 127, 0) - down, 1)
    scale = np.exp2(byte - 127.0)
    codes = (blocks / scale).astype(np.float32).astype(dtype).astype(np.float64)
    return np.moveaxis((codes * scale).reshape(v.shape), -1, axis)


WIDE = False


def mx_kscale(k):
    if not WIDE:
        return np.ones(k)
    levels = np.array([10, -10, 5, -5, 0])
    if k % 512:
        return np.exp2(np.random.permutation(np.resize(levels, k // 32))).repeat(32)
    a = np.empty((k // 512, 16))
    for p in range(k // 512):
        a[p, :8] = np.random.permutation(np.resize(levels, 8))
        for g in range(8):
            far = levels[np.abs(levels - a[p, g]) >= 10]
            a[p, g + 8] = far[np.random.randint(len(far))]
    return np.exp2(a.ravel()).repeat(32)


def f64(x):
    return np.asarray(x).astype(np.float64)


def striped(idx):
    return np.tile(idx.reshape(-1, 16).T, (8, 1)).astype(np.uint16)


def unstriped(offs):
    return offs[:16].T.reshape(-1).astype(np.int64)


E2M1 = np.array([0.0, 0.5, 1.0, 1.5, 2.0, 3.0, 4.0, 6.0, -0.0, -0.5, -1.0, -1.5, -2.0, -3.0, -4.0, -6.0])


def pack_weight(w, fmt):
    k, n = w.shape
    w = f64(np.asarray(w, np.float32).astype(ml_dtypes.bfloat16)).reshape(k // 32, 32, n)
    amax = np.abs(w).max(1)
    if fmt == "e4m3":
        byte = np.frexp(amax)[1] - 1 + 127 - 7
    else:
        mant, ex = np.frexp(amax / 6.0)
        byte = np.where(mant > 0.5, ex, ex - 1) + 127
    byte = np.clip(np.where(amax > 0, byte, 1), 1, 254)
    scaled = (w * np.exp2(127.0 - byte)[:, None, :]).reshape(k, n).astype(np.float32)
    by_word = np.ascontiguousarray(scaled.reshape(k // 512, 128, 4, n).transpose(0, 1, 3, 2))
    if fmt == "e4m3":
        words = by_word.astype(ml_dtypes.float8_e4m3fn).view(np.uint8)
    else:
        c = by_word.astype(ml_dtypes.float4_e2m1fn).view(np.uint8) & 0xF
        words = (c[..., 0::2] | (c[..., 1::2] << 4)).reshape(k // 512, 128, 2 * n)
    return np.ascontiguousarray(words), np.ascontiguousarray(byte.astype(np.uint8).reshape(k // 512, 16, n))


def unpack_weight(words, scales, fmt):
    g, _, n = scales.shape
    words = np.ascontiguousarray(words).reshape(g, 128, n, -1)
    if fmt == "e4m3":
        vals = words.view(ml_dtypes.float8_e4m3fn).astype(np.float64)
    else:
        nib = np.empty((g, 128, n, 4), np.uint8)
        nib[..., 0::2] = words & 0xF
        nib[..., 1::2] = words >> 4
        vals = E2M1[nib]
    vals = vals * np.repeat(np.exp2(scales.astype(np.float64) - 127.0), 8, axis=1)[..., None]
    return vals.transpose(0, 1, 3, 2).reshape(g * 512, n)


def relu(v):
    return np.maximum(v, 0.0)


K, T, E, C, N = 2048, 768, 6, 128, 128
TOP = 3
PAD = 64
K8 = 1024


def by_expert(wq, xq):
    return np.concatenate([wq[e].T @ xq[:, e * C:(e + 1) * C] for e in range(E)], axis=1)


def setup_inputs():
    n = np.random.standard_normal
    s = mx_kscale(K)[:, None]
    slot_token = np.empty(E * C, np.int64); pos = np.tile(E * C + np.arange(T) % PAD, (TOP, 1)); taken = np.zeros(T, np.int64)
    liked = np.random.randn(T)
    for e in np.random.permutation(E):
        free = np.flatnonzero(taken < TOP); pick = np.random.permutation(free[np.argsort(-(liked[free] + np.random.gumbel(size=free.size)))[:C]]); slot_token[e * C:(e + 1) * C] = pick
        pos[taken[pick], pick] = e * C + np.arange(C); taken[pick] += 1
    g = np.random.uniform(0.2, 0.8, (TOP, T))
    w = n((E, K, N)) / np.sqrt(K) / s[None]
    w8 = [pack_weight(m[:K8], "e4m3") for m in w]
    w4 = [pack_weight(m[K8:], "e2m1") for m in w]
    return {
        "xT": (n((K, T)) * s).astype(np.float32),
        "w8_words": np.stack([m[0] for m in w8]),
        "w8_scales": np.stack([m[1] for m in w8]),
        "w4_words": np.stack([m[0] for m in w4]),
        "w4_scales": np.stack([m[1] for m in w4]),
        "b": (0.3 * n((N, E))).astype(np.float32),
        "gate": np.stack([np.tile(r, (N, 1)) for r in g]).astype(np.float32),
        "offs": striped(slot_token),
        "pos1": striped(pos[0]),
        "pos2": striped(pos[1]),
        "pos3": striped(pos[2]),
    }


def reference(xT, w8_words, w8_scales, w4_words, w4_scales, b, gate, offs, pos1, pos2, pos3):
    idx = unstriped(offs)
    w = np.stack([np.concatenate([unpack_weight(w8_words[e], w8_scales[e], "e4m3"), unpack_weight(w4_words[e], w4_scales[e], "e2m1")]) for e in range(E)])
    xq = mxq(f64(xT)[:, idx], 0, "e4m3")
    y = by_expert(w, xq)
    y = relu(y + np.repeat(f64(b), C, axis=1))
    y = np.concatenate([y, np.zeros((N, PAD))], axis=1)
    return sum(f64(gate[r]) * y[:, unstriped(p)] for r, p in enumerate((pos1, pos2, pos3)))

@@ -1,0 +1,185 @@
+from contextlib import ExitStack
+
+import concourse.mybir as mybir
+
+K, T, E, C, N = 2048, 768, 6, 128, 128
+TOP = 3
+PAD = 64
+S = E * C
+FLOPS = 2 * K * N * S
+
+F32 = mybir.dt.float32
+BF16 = mybir.dt.bfloat16
+I32 = mybir.dt.int32
+U32 = mybir.dt.uint32
+U16 = mybir.dt.uint16
+U8 = mybir.dt.uint8
+FP8X4 = mybir.dt.float8_e4m3fn_x4
+FP4X4 = mybir.dt.float4_e2m1fn_x4
+COPY = mybir.ActivationFunctionType.Copy
+RELU = mybir.ActivationFunctionType.Relu
+MULT = mybir.AluOpType.mult
+ADD = mybir.AluOpType.add
+
+P = 128
+PACK = 4
+K_PASS = P * PACK
+CHUNK = 256
+CHUNKS = T // CHUNK
+PASSES = [(2, 0, 0), (0, 1, 4), (1, 1, 8), (3, 1, 0)]
+LAST_CUTS = [0, 384, 640, 768]
+OUT_CUTS = [0, 384, 640, 768]
+
+
+def cols(lst, a, b):
+    return lst[:, a // 16 : b // 16]
+
+
+def tile_moe_ecr_lin_relu_kernel(
+    tc, xT, w8_words, w8_scales, w4_words, w4_scales, b, gate, offs, pos1, pos2, pos3, out
+):
+    nc = tc.nc
+    with ExitStack() as ctx:
+        keep = ctx.enter_context(tc.tile_pool(name="keep", bufs=1))
+        psum = ctx.enter_context(tc.psum_pool(name="psum", bufs=1))
+
+        offs_t = keep.tile([P, S // 16], U16, name="offs_t")
+        pos_t = [keep.tile([P, T // 16], U16, name="pos%d" % r) for r in range(TOP)]
+        codes = [keep.tile([P, T], U32, name="codes%d" % i, align_bytes=64) for i in range(4)]
+        planes = [keep.tile([P, T], U8, name="planes%d" % i, align_bytes=64) for i in range(2)]
+        g_codes = [keep.tile([P, S], U32, name="gcodes%d" % i, align_bytes=64) for i in range(4)]
+        g_planes = [keep.tile([P, S], U8, name="gplanes%d" % i, align_bytes=64) for i in range(2)]
+        w8 = [keep.tile([P, E, 4 * N], U8, name="w8_%d" % h, align_bytes=64) for h in range(2)]
+        w4 = [keep.tile([P, E, 2 * N], U8, name="w4_%d" % h, align_bytes=64) for h in range(2)]
+        ws8 = keep.tile([P, 2 * E, N], U8, name="ws8", align_bytes=64)
+        ws4 = keep.tile([P, 2 * E, N], U8, name="ws4", align_bytes=64)
+        bias = keep.tile([P, E], F32, name="bias")
+        y = keep.tile([P, S + PAD], F32, name="y")
+        banks = [psum.tile([P, C], F32, name="bank%d" % e) for e in range(E)]
+
+        raw = {}
+        for i, (a, pl, k0) in enumerate(PASSES):
+            for c in range(CHUNKS):
+                raw[i, c] = keep.tile([P, PACK, CHUNK], F32, name="raw%d_%d" % (i, c))
+                nc.sync.dma_start(
+                    out=raw[i, c][:],
+                    in_=xT[a * K_PASS : (a + 1) * K_PASS, c * CHUNK : (c + 1) * CHUNK].rearrange(
+                        "(p j) w -> p j w", j=PACK
+                    ),
+                )
+                if i == 0 and c == CHUNKS - 1:
+                    nc.sync.dma_start(offs_t[:], offs)
+
+        for pl in planes:
+            nc.vector.memset(pl[:].bitcast(I32), 0)
+        nc.vector.memset(ws8[:].rearrange("p a n -> p (a n)").bitcast(I32), 0)
+        nc.vector.memset(ws4[:].rearrange("p a n -> p (a n)").bitcast(I32), 0)
+        nc.vector.memset(y[:, S:], 0.0)
+
+        for dst, src in ((ws4, w4_scales), (ws8, w8_scales)):
+            rows = src.rearrange("e a (q r) n -> r q (e a) n", r=4)
+            for r in range(4):
+                nc.sync.dma_start(out=dst[r:P:32, :, :].bitcast(I32), in_=rows[r].bitcast(I32))
+        w8v = w8_words.rearrange("(h e) a p n r -> h p (e a) (n r)", h=2)
+        w4v = w4_words.rearrange("(h e) a p m -> h p (e a) m", h=2)
+        for h in range(2):
+            nc.sync.dma_start(out=w4[h][:].bitcast(I32), in_=w4v[h].bitcast(I32))
+            nc.sync.dma_start(out=w8[h][:].bitcast(I32), in_=w8v[h].bitcast(I32))
+        nc.sync.dma_start(out=bias[:], in_=b)
+        for r, lst in enumerate((pos1, pos2, pos3)):
+            nc.sync.dma_start(pos_t[r][:], lst)
+        gates = []
+        for j in range(len(OUT_CUTS) - 1):
+            t0, t1 = OUT_CUTS[j], OUT_CUTS[j + 1]
+            g = keep.tile([P, TOP, t1 - t0], F32, name="gate%d" % j)
+            nc.sync.dma_start(out=g[:], in_=gate[:, :, t0:t1].rearrange("r p t -> p r t"))
+            gates.append(g)
+
+        def multiply(i, e):
+            a, pl, k0 = PASSES[i]
+            if a < 2:
+                lhsT = w8[e // 3][:, 2 * (e % 3) + a, :].bitcast(FP8X4)
+                lhsT_scale = ws8[:, 2 * e + a, :]
+            else:
+                lhsT = w4[e // 3][:, 2 * (e % 3) + a - 2, :].bitcast(FP4X4)
+                lhsT_scale = ws4[:, 2 * e + a - 2, :]
+            sl = slice(e * C, (e + 1) * C)
+            nc.tensor.matmul_mx(
+                out=banks[e][:],
+                lhsT=lhsT,
+                lhsT_scale=lhsT_scale,
+                rhs=g_codes[i][:, sl].bitcast(FP8X4),
+                rhs_scale=g_planes[pl][k0:P, sl],
+                start=(i == 0),
+                stop=(i == 3),
+            )
+
+        def cast(engine_is_vector, i, c, w0, w1):
+            gr = keep.tile([P, w1 - w0, PACK], BF16, name="grouped%d_%d_%d" % (i, c, w0), align_bytes=64)
+            dst = gr[:].rearrange("p (c i) t -> p c t i", i=4)
+            src = raw[i, c][:, :, w0:w1].rearrange("p t (c i) -> p c t i", i=4)
+            if engine_is_vector:
+                nc.vector.tensor_copy(out=dst, in_=src)
+            else:
+                nc.scalar.activation(dst, src, COPY)
+            return gr, c * CHUNK + w0, c * CHUNK + w1
+
+        def quantise(i, piece):
+            gr, t0, t1 = piece
+            a, pl, k0 = PASSES[i]
+            nc.vector.quantize_mx(
+                out=codes[i][:, t0:t1].bitcast(FP8X4),
+                scales=planes[pl][k0:P, t0:t1],
+                in_=gr[:].rearrange("p w j -> p (w j)"),
+            )
+
+        def gather(dst, src, s0, s1):
+            nc.vector.tensor_copy(dst[:, s0:s1], src[:].indirect(cols(offs_t, s0, s1)))
+
+        for i in range(4):
+            pieces = []
+            for c in range(CHUNKS):
+                if i == 0:
+                    pieces.append(cast(True, i, c, 0, CHUNK))
+                elif i >= 2 and c == CHUNKS - 1:
+                    pieces.append(cast(False, i, c, 0, CHUNK // 2))
+                    pieces.append(cast(True, i, c, CHUNK // 2, CHUNK))
+                else:
+                    pieces.append(cast(False, i, c, 0, CHUNK))
+                if i == 0 and c > 0:
+                    quantise(i, pieces[c - 1])
+            for piece in pieces[CHUNKS - 1 :] if i == 0 else pieces:
+                quantise(i, piece)
+            if i < 3:
+                for h in range(2):
+                    gather(g_codes[i], codes[i], h * S // 2, (h + 1) * S // 2)
+            if i == 0:
+                for h in range(2):
+                    gather(g_planes[0], planes[0], h * S // 2, (h + 1) * S // 2)
+        for h in range(2):
+            gather(g_planes[1], planes[1], h * S // 2, (h + 1) * S // 2)
+            for e in range(3 * h, 3 * h + 3):
+                for i in range(3):
+                    multiply(i, e)
+        for j in range(len(LAST_CUTS) - 1):
+            s0, s1 = LAST_CUTS[j], LAST_CUTS[j + 1]
+            gather(g_codes[3], codes[3], s0, s1)
+            for e in range(s0 // C, s1 // C):
+                multiply(3, e)
+                nc.scalar.activation(y[:, e * C : (e + 1) * C], banks[e][:], RELU, bias=bias[:, e : e + 1])
+
+        pending = None
+        for j in range(len(OUT_CUTS) - 1):
+            t0, t1 = OUT_CUTS[j], OUT_CUTS[j + 1]
+            parts = [keep.tile([P, t1 - t0], F32, name="part%d_%d" % (j, r)) for r in range(TOP)]
+            pair = keep.tile([P, t1 - t0], F32, name="pair%d" % j)
+            total = keep.tile([P, t1 - t0], F32, name="total%d" % j)
+            for r in range(TOP):
+                nc.vector.tensor_tensor(parts[r][:], y[:].indirect(cols(pos_t[r], t0, t1)), gates[j][:, r, :], MULT)
+                if r == 0 and pending is not None:
+                    nc.vector.tensor_tensor(pending[0][:], pending[1][:], pending[2][:], ADD)
+                    nc.sync.dma_start(out=out[:, pending[3] : pending[4]], in_=pending[0][:])
+            nc.vector.tensor_tensor(pair[:], parts[0][:], parts[1][:], ADD)
+            pending = (total, pair, parts[2], t0, t1)
+        nc.vector.tensor_tensor(pending[0][:], pending[1][:], pending[2][:], ADD)
+        nc.sync.dma_start(out=out[:, pending[3] : pending[4]], in_=pending[0][:])

@@ -1,6 +1,7 @@
 from contextlib import ExitStack
 
 import concourse.mybir as mybir
+from concourse.masks import make_identity
 
 K, T, E, C, N = 2048, 768, 6, 128, 128
 TOP = 3
@@ -20,15 +21,22 @@ COPY = mybir.ActivationFunctionType.Copy
 RELU = mybir.ActivationFunctionType.Relu
 MULT = mybir.AluOpType.mult
 ADD = mybir.AluOpType.add
+MAX = mybir.AluOpType.max
 
 P = 128
 PACK = 4
 K_PASS = P * PACK
 CHUNK = 256
 CHUNKS = T // CHUNK
+WINDOW = 1024
 PASSES = [(2, 0, 0), (0, 1, 4), (1, 1, 8), (3, 1, 0)]
-LAST_CUTS = [0, 384, 640, 768]
-OUT_CUTS = [0, 384, 640, 768]
+LOADS = [[(0, 512), (512, 768)]] + [[(0, 256), (256, 512), (512, 768)]] * 3
+CASTS = [
+    [(True, 0, 256), (False, 256, 512), (True, 512, 640), (False, 640, 768)],
+    [(False, 0, 256), (False, 256, 512), (False, 512, 768)],
+    [(False, 0, 256), (False, 256, 512), (False, 512, 768)],
+    [(False, 0, 256), (False, 256, 512), (False, 512, 768)],
+]
 
 
 def cols(lst, a, b):
@@ -45,55 +53,67 @@ def tile_moe_ecr_lin_relu_kernel(
 
         offs_t = keep.tile([P, S // 16], U16, name="offs_t")
         pos_t = [keep.tile([P, T // 16], U16, name="pos%d" % r) for r in range(TOP)]
-        codes = [keep.tile([P, T], U32, name="codes%d" % i, align_bytes=64) for i in range(4)]
-        planes = [keep.tile([P, T], U8, name="planes%d" % i, align_bytes=64) for i in range(2)]
+        codes = [keep.tile([P, WINDOW], I32, name="codes%d" % i, align_bytes=64) for i in range(4)]
+        planes = [keep.tile([P, WINDOW], U8, name="planes%d" % i, align_bytes=64) for i in range(2)]
         g_codes = [keep.tile([P, S], U32, name="gcodes%d" % i, align_bytes=64) for i in range(4)]
-        g_planes = [keep.tile([P, S], U8, name="gplanes%d" % i, align_bytes=64) for i in range(2)]
+        g_shared = keep.tile([P, S], U8, name="g_shared", align_bytes=64)
+        g_lone = []
         w8 = [keep.tile([P, E, 4 * N], U8, name="w8_%d" % h, align_bytes=64) for h in range(2)]
         w4 = [keep.tile([P, E, 2 * N], U8, name="w4_%d" % h, align_bytes=64) for h in range(2)]
         ws8 = keep.tile([P, 2 * E, N], U8, name="ws8", align_bytes=64)
         ws4 = keep.tile([P, 2 * E, N], U8, name="ws4", align_bytes=64)
         bias = keep.tile([P, E], F32, name="bias")
         y = keep.tile([P, S + PAD], F32, name="y")
-        banks = [psum.tile([P, C], F32, name="bank%d" % e) for e in range(E)]
+        ident = keep.tile([P, P], F32, name="ident")
+        banks = [psum.tile([P, C], F32, name="bank%d" % e, tag="bank%d" % e) for e in range(E)]
+        raw = {
+            (i, t0): keep.tile([P, PACK, t1 - t0], F32, name="raw%d_%d" % (i, t0), tag="raw%d_%d" % (i, t0), align_bytes=64)
+            for i in range(4)
+            for t0, t1 in LOADS[i]
+        }
+        gates = [keep.tile([P, TOP, CHUNK], F32, name="gate%d" % j) for j in range(CHUNKS)]
 
-        raw = {}
-        for i, (a, pl, k0) in enumerate(PASSES):
-            for c in range(CHUNKS):
-                raw[i, c] = keep.tile([P, PACK, CHUNK], F32, name="raw%d_%d" % (i, c))
-                nc.sync.dma_start(
-                    out=raw[i, c][:],
-                    in_=xT[a * K_PASS : (a + 1) * K_PASS, c * CHUNK : (c + 1) * CHUNK].rearrange(
-                        "(p j) w -> p j w", j=PACK
-                    ),
-                )
-                if i == 0 and c == CHUNKS - 1:
-                    nc.sync.dma_start(offs_t[:], offs)
-
+        nc.vector.memset(ws4[:].rearrange("p a n -> p (a n)").bitcast(I32), 0)
+        nc.vector.memset(ws8[:].rearrange("p a n -> p (a n)").bitcast(I32), 0)
         for pl in planes:
             nc.vector.memset(pl[:].bitcast(I32), 0)
-        nc.vector.memset(ws8[:].rearrange("p a n -> p (a n)").bitcast(I32), 0)
-        nc.vector.memset(ws4[:].rearrange("p a n -> p (a n)").bitcast(I32), 0)
+        for cd in codes:
+            nc.vector.memset(cd[:, T:], 0)
         nc.vector.memset(y[:, S:], 0.0)
+        make_identity(nc, ident[:])
 
-        for dst, src in ((ws4, w4_scales), (ws8, w8_scales)):
+        def load_x(i, t0, t1):
+            a = PASSES[i][0]
+            nc.sync.dma_start(
+                out=raw[i, t0][:],
+                in_=xT[a * K_PASS : (a + 1) * K_PASS, t0:t1].rearrange("(p j) w -> p j w", j=PACK),
+            )
+
+        def load_scales(dst, src, r):
             rows = src.rearrange("e a (q r) n -> r q (e a) n", r=4)
-            for r in range(4):
-                nc.sync.dma_start(out=dst[r:P:32, :, :].bitcast(I32), in_=rows[r].bitcast(I32))
+            nc.sync.dma_start(out=dst[r:P:32, :, :].bitcast(I32), in_=rows[r].bitcast(I32))
+
         w8v = w8_words.rearrange("(h e) a p n r -> h p (e a) (n r)", h=2)
-        w4v = w4_words.rearrange("(h e) a p m -> h p (e a) m", h=2)
+        w4v = w4_words.rearrange("e a p m -> a p e m")
+
+        for i in range(4):
+            for t0, t1 in LOADS[i]:
+                load_x(i, t0, t1)
+            if i == 0:
+                nc.sync.dma_start(offs_t[:], offs)
+        for r in range(4):
+            load_scales(ws4, w4_scales, r)
+        nc.sync.dma_start(out=w4[0][:].bitcast(I32), in_=w4v[0].bitcast(I32))
+        for r in range(4):
+            load_scales(ws8, w8_scales, r)
         for h in range(2):
-            nc.sync.dma_start(out=w4[h][:].bitcast(I32), in_=w4v[h].bitcast(I32))
             nc.sync.dma_start(out=w8[h][:].bitcast(I32), in_=w8v[h].bitcast(I32))
-        nc.sync.dma_start(out=bias[:], in_=b)
+        nc.sync.dma_start(out=w4[1][:].bitcast(I32), in_=w4v[1].bitcast(I32))
+        nc.sync.dma_start(bias[:], b)
         for r, lst in enumerate((pos1, pos2, pos3)):
             nc.sync.dma_start(pos_t[r][:], lst)
-        gates = []
-        for j in range(len(OUT_CUTS) - 1):
-            t0, t1 = OUT_CUTS[j], OUT_CUTS[j + 1]
-            g = keep.tile([P, TOP, t1 - t0], F32, name="gate%d" % j)
-            nc.sync.dma_start(out=g[:], in_=gate[:, :, t0:t1].rearrange("r p t -> p r t"))
-            gates.append(g)
+        for j in range(CHUNKS):
+            nc.sync.dma_start(out=gates[j][:], in_=gate[:, :, j * CHUNK : (j + 1) * CHUNK].rearrange("r p t -> p r t"))
 
         def multiply(i, e):
             a, pl, k0 = PASSES[i]
@@ -101,7 +121,7 @@ def tile_moe_ecr_lin_relu_kernel(
                 lhsT = w8[e // 3][:, 2 * (e % 3) + a, :].bitcast(FP8X4)
                 lhsT_scale = ws8[:, 2 * e + a, :]
             else:
-                lhsT = w4[e // 3][:, 2 * (e % 3) + a - 2, :].bitcast(FP4X4)
+                lhsT = w4[a - 2][:, e, :].bitcast(FP4X4)
                 lhsT_scale = ws4[:, 2 * e + a - 2, :]
             sl = slice(e * C, (e + 1) * C)
             nc.tensor.matmul_mx(
@@ -109,23 +129,23 @@ def tile_moe_ecr_lin_relu_kernel(
                 lhsT=lhsT,
                 lhsT_scale=lhsT_scale,
                 rhs=g_codes[i][:, sl].bitcast(FP8X4),
-                rhs_scale=g_planes[pl][k0:P, sl],
+                rhs_scale=g_shared[k0:P, sl] if pl == 1 else g_lone[e // 2][:, (e % 2) * C : (e % 2 + 1) * C],
                 start=(i == 0),
                 stop=(i == 3),
             )
 
-        def cast(engine_is_vector, i, c, w0, w1):
-            gr = keep.tile([P, w1 - w0, PACK], BF16, name="grouped%d_%d_%d" % (i, c, w0), align_bytes=64)
+        def cast(i, on_vector, t0, t1):
+            l0 = max(a for a, z in LOADS[i] if a <= t0)
+            gr = keep.tile([P, t1 - t0, PACK], BF16, name="grouped%d_%d" % (i, t0), align_bytes=64)
             dst = gr[:].rearrange("p (c i) t -> p c t i", i=4)
-            src = raw[i, c][:, :, w0:w1].rearrange("p t (c i) -> p c t i", i=4)
-            if engine_is_vector:
+            src = raw[i, l0][:, :, t0 - l0 : t1 - l0].rearrange("p t (c i) -> p c t i", i=4)
+            if on_vector:
                 nc.vector.tensor_copy(out=dst, in_=src)
             else:
                 nc.scalar.activation(dst, src, COPY)
-            return gr, c * CHUNK + w0, c * CHUNK + w1
+            return gr
 
-        def quantise(i, piece):
-            gr, t0, t1 = piece
+        def quantise(i, t0, t1, gr):
             a, pl, k0 = PASSES[i]
             nc.vector.quantize_mx(
                 out=codes[i][:, t0:t1].bitcast(FP8X4),
@@ -133,53 +153,62 @@ def tile_moe_ecr_lin_relu_kernel(
                 in_=gr[:].rearrange("p w j -> p (w j)"),
             )
 
-        def gather(dst, src, s0, s1):
-            nc.vector.tensor_copy(dst[:, s0:s1], src[:].indirect(cols(offs_t, s0, s1)))
+        def gather(dst, window, s0, s1):
+            nc.vector.tensor_copy(dst[:, s0:s1], window.indirect(cols(offs_t, s0, s1)))
 
         for i in range(4):
-            pieces = []
-            for c in range(CHUNKS):
-                if i == 0:
-                    pieces.append(cast(True, i, c, 0, CHUNK))
-                elif i >= 2 and c == CHUNKS - 1:
-                    pieces.append(cast(False, i, c, 0, CHUNK // 2))
-                    pieces.append(cast(True, i, c, CHUNK // 2, CHUNK))
-                else:
-                    pieces.append(cast(False, i, c, 0, CHUNK))
-                if i == 0 and c > 0:
-                    quantise(i, pieces[c - 1])
-            for piece in pieces[CHUNKS - 1 :] if i == 0 else pieces:
-                quantise(i, piece)
-            if i < 3:
-                for h in range(2):
-                    gather(g_codes[i], codes[i], h * S // 2, (h + 1) * S // 2)
+            pieces = [(t0, t1, cast(i, v, t0, t1)) for v, t0, t1 in CASTS[i]]
+            for t0, t1, gr in pieces:
+                quantise(i, t0, t1, gr)
             if i == 0:
-                for h in range(2):
-                    gather(g_planes[0], planes[0], h * S // 2, (h + 1) * S // 2)
+                gather(g_codes[i], codes[i][:].bitcast(U32), 0, S)
+            if i < 3:
+                tag = "g_lone" if i == 0 else "raw%d_%d" % (i, LOADS[i][-1][0])
+                g_lone.append(keep.tile([P, 2 * C], U8, name="g_lone%d" % i, tag=tag, align_bytes=64))
+                nc.vector.tensor_copy(g_lone[i][:], planes[0][:].indirect(cols(offs_t, 2 * C * i, 2 * C * (i + 1))))
+            if i in (1, 2):
+                gather(g_codes[i], codes[i][:].bitcast(U32), 0, S)
+        for e in range(E):
+            multiply(0, e)
         for h in range(2):
-            gather(g_planes[1], planes[1], h * S // 2, (h + 1) * S // 2)
+            gather(g_shared, planes[1][:], h * S // 2, (h + 1) * S // 2)
             for e in range(3 * h, 3 * h + 3):
-                for i in range(3):
+                for i in (1, 2):
                     multiply(i, e)
-        for j in range(len(LAST_CUTS) - 1):
-            s0, s1 = LAST_CUTS[j], LAST_CUTS[j + 1]
-            gather(g_codes[3], codes[3], s0, s1)
-            for e in range(s0 // C, s1 // C):
+        for group in ((0, 1, 2), (3, 4), (5,)):
+            gather(g_codes[3], codes[3][:].bitcast(U32), group[0] * C, (group[-1] + 1) * C)
+            for e in group:
                 multiply(3, e)
-                nc.scalar.activation(y[:, e * C : (e + 1) * C], banks[e][:], RELU, bias=bias[:, e : e + 1])
+                if e < E - 1:
+                    nc.scalar.activation(y[:, e * C : (e + 1) * C], banks[e][:], RELU, bias=bias[:, e : e + 1])
+                else:
+                    nc.vector.tensor_scalar(y[:, e * C : (e + 1) * C], banks[e][:], bias[:, e : e + 1], 0.0, ADD, MAX)
 
-        pending = None
-        for j in range(len(OUT_CUTS) - 1):
-            t0, t1 = OUT_CUTS[j], OUT_CUTS[j + 1]
-            parts = [keep.tile([P, t1 - t0], F32, name="part%d_%d" % (j, r)) for r in range(TOP)]
-            pair = keep.tile([P, t1 - t0], F32, name="pair%d" % j)
-            total = keep.tile([P, t1 - t0], F32, name="total%d" % j)
+        free = ["spare0", "spare1", "bank0", "bank1", "bank2", "bank3"]
+        for j in range(CHUNKS):
+            t0, t1 = j * CHUNK, (j + 1) * CHUNK
+            parts = [keep.tile([P, CHUNK], F32, name="part%d_%d" % (j, r)) for r in range(TOP)]
+            total = keep.tile([P, CHUNK], F32, name="total%d" % j)
+            on_tensor = j < CHUNKS - 1
+            if on_tensor:
+                sums = [psum.tile([P, P], F32, name="sum%d_%d" % (j, u), tag=free[3 * j + u]) for u in range(2)]
             for r in range(TOP):
                 nc.vector.tensor_tensor(parts[r][:], y[:].indirect(cols(pos_t[r], t0, t1)), gates[j][:, r, :], MULT)
-                if r == 0 and pending is not None:
-                    nc.vector.tensor_tensor(pending[0][:], pending[1][:], pending[2][:], ADD)
-                    nc.sync.dma_start(out=out[:, pending[3] : pending[4]], in_=pending[0][:])
-            nc.vector.tensor_tensor(pair[:], parts[0][:], parts[1][:], ADD)
-            pending = (total, pair, parts[2], t0, t1)
-        nc.vector.tensor_tensor(pending[0][:], pending[1][:], pending[2][:], ADD)
-        nc.sync.dma_start(out=out[:, pending[3] : pending[4]], in_=pending[0][:])
+                if on_tensor:
+                    for u in range(2):
+                        nc.tensor.matmul(
+                            sums[u][:], parts[r][:, u * P : (u + 1) * P], ident[:],
+                            start=(r == 0), stop=(r == TOP - 1), is_transpose=True,
+                        )
+            if on_tensor:
+                turned = keep.tile([P, 2, P], F32, name="turned%d" % j)
+                back = psum.tile([P, CHUNK], F32, name="back%d" % j, tag=free[3 * j + 2])
+                for u in range(2):
+                    nc.scalar.copy(turned[:, u, :], sums[u][:])
+                    nc.tensor.transpose(back[:, u * P : (u + 1) * P], turned[:, u, :], ident[:])
+                nc.scalar.copy(total[:], back[:])
+            else:
+                pair = keep.tile([P, CHUNK], F32, name="pair%d" % j)
+                nc.vector.tensor_tensor(pair[:], parts[0][:], parts[1][:], ADD)
+                nc.vector.tensor_tensor(total[:], pair[:], parts[2][:], ADD)
+            nc.sync.dma_start(out=out[:, t0:t1], in_=total[:])

@@ -26,21 +26,23 @@ MAX = mybir.AluOpType.max
 P = 128
 PACK = 4
 K_PASS = P * PACK
+FP8_PASSES = 2
+QUADRANT = 32
+ROWS = 4
+LIST_ROWS = 16
 CHUNK = 256
 CHUNKS = T // CHUNK
 WINDOW = 1024
-PASSES = [(2, 0, 0), (0, 1, 4), (1, 1, 8), (3, 1, 0)]
-LOADS = [[(0, 512), (512, 768)]] + [[(0, 256), (256, 512), (512, 768)]] * 3
-CASTS = [
-    [(True, 0, 256), (False, 256, 512), (True, 512, 640), (False, 640, 768)],
-    [(False, 0, 256), (False, 256, 512), (False, 512, 768)],
-    [(False, 0, 256), (False, 256, 512), (False, 512, 768)],
-    [(False, 0, 256), (False, 256, 512), (False, 512, 768)],
-]
+
+STEPS = ((2, 0), (0, 4), (1, 8), (3, 0))
+LAST = len(STEPS) - 1
+LOADS = [[(0, 2 * CHUNK), (2 * CHUNK, T)]] + [[(t, t + CHUNK) for t in range(0, T, CHUNK)]] * LAST
+SHARE = 112
+GROUPS = ((0, 1, 2), (3, 4), (5,))
 
 
-def cols(lst, a, b):
-    return lst[:, a // 16 : b // 16]
+def entries(lst, first, end):
+    return lst[:, first // LIST_ROWS : end // LIST_ROWS]
 
 
 def tile_moe_ecr_lin_relu_kernel(
@@ -51,164 +53,190 @@ def tile_moe_ecr_lin_relu_kernel(
         keep = ctx.enter_context(tc.tile_pool(name="keep", bufs=1))
         psum = ctx.enter_context(tc.psum_pool(name="psum", bufs=1))
 
-        offs_t = keep.tile([P, S // 16], U16, name="offs_t")
-        pos_t = [keep.tile([P, T // 16], U16, name="pos%d" % r) for r in range(TOP)]
-        codes = [keep.tile([P, WINDOW], I32, name="codes%d" % i, align_bytes=64) for i in range(4)]
-        planes = [keep.tile([P, WINDOW], U8, name="planes%d" % i, align_bytes=64) for i in range(2)]
-        g_codes = [keep.tile([P, S], U32, name="gcodes%d" % i, align_bytes=64) for i in range(4)]
-        g_shared = keep.tile([P, S], U8, name="g_shared", align_bytes=64)
-        g_lone = []
-        w8 = [keep.tile([P, E, 4 * N], U8, name="w8_%d" % h, align_bytes=64) for h in range(2)]
-        w4 = [keep.tile([P, E, 2 * N], U8, name="w4_%d" % h, align_bytes=64) for h in range(2)]
-        ws8 = keep.tile([P, 2 * E, N], U8, name="ws8", align_bytes=64)
-        ws4 = keep.tile([P, 2 * E, N], U8, name="ws4", align_bytes=64)
+        offs_t = keep.tile([P, S // LIST_ROWS], U16, name="offs_t")
+        pos_t = [keep.tile([P, T // LIST_ROWS], U16, name="pos%d" % r) for r in range(TOP)]
+        words = [keep.tile([P, WINDOW], I32, name="words%d" % i, align_bytes=64) for i in range(len(STEPS))]
+        lone_plane = keep.tile([P, WINDOW], U8, name="lone_plane", align_bytes=64)
+        shared_planes = keep.tile([P, WINDOW], U8, name="shared_planes", align_bytes=64)
+        slot_words = [keep.tile([P, S], U32, name="slot_words%d" % i, align_bytes=64) for i in range(len(STEPS))]
+        slot_shared = keep.tile([P, S], U8, name="slot_shared", align_bytes=64)
+        slot_lone = []
+        w8 = [keep.tile([P, FP8_PASSES * len(g), 4 * N], U8, name="w8_%d" % g[0], align_bytes=64) for g in GROUPS]
+        w4 = [keep.tile([P, E, 2 * N], U8, name="w4_%d" % a, align_bytes=64) for a in range(2)]
+        w8_planes = keep.tile([P, 2 * E, N], U8, name="w8_planes", align_bytes=64)
+        w4_planes = keep.tile([P, 2 * E, N], U8, name="w4_planes", align_bytes=64)
         bias = keep.tile([P, E], F32, name="bias")
         y = keep.tile([P, S + PAD], F32, name="y")
         ident = keep.tile([P, P], F32, name="ident")
         banks = [psum.tile([P, C], F32, name="bank%d" % e, tag="bank%d" % e) for e in range(E)]
         raw = {
-            (i, t0): keep.tile([P, PACK, t1 - t0], F32, name="raw%d_%d" % (i, t0), tag="raw%d_%d" % (i, t0), align_bytes=64)
-            for i in range(4)
+            (i, t0): keep.tile(
+                [P, PACK, t1 - t0], F32, name="raw%d_%d" % (i, t0), tag="raw%d_%d" % (i, t0), align_bytes=64
+            )
+            for i in range(len(STEPS))
             for t0, t1 in LOADS[i]
         }
         gates = [keep.tile([P, TOP, CHUNK], F32, name="gate%d" % j) for j in range(CHUNKS)]
 
-        nc.vector.memset(ws4[:].rearrange("p a n -> p (a n)").bitcast(I32), 0)
-        nc.vector.memset(ws8[:].rearrange("p a n -> p (a n)").bitcast(I32), 0)
-        for pl in planes:
-            nc.vector.memset(pl[:].bitcast(I32), 0)
-        for cd in codes:
-            nc.vector.memset(cd[:, T:], 0)
+        nc.vector.memset(w4_planes[:].rearrange("p a n -> p (a n)").bitcast(I32), 0)
+        nc.vector.memset(w8_planes[:].rearrange("p a n -> p (a n)").bitcast(I32), 0)
+        for plane in (lone_plane, shared_planes):
+            nc.vector.memset(plane[:].bitcast(I32), 0)
+        for step_words in words:
+            nc.vector.memset(step_words[:, T:], 0)
         nc.vector.memset(y[:, S:], 0.0)
         make_identity(nc, ident[:])
 
-        def load_x(i, t0, t1):
-            a = PASSES[i][0]
-            nc.sync.dma_start(
-                out=raw[i, t0][:],
-                in_=xT[a * K_PASS : (a + 1) * K_PASS, t0:t1].rearrange("(p j) w -> p j w", j=PACK),
-            )
+        def load_bytes(dst, src):
+            nc.sync.dma_start(out=dst.bitcast(I32), in_=src.bitcast(I32))
 
-        def load_scales(dst, src, r):
-            rows = src.rearrange("e a (q r) n -> r q (e a) n", r=4)
-            nc.sync.dma_start(out=dst[r:P:32, :, :].bitcast(I32), in_=rows[r].bitcast(I32))
+        def load_planes(dst, src):
+            rows = src.rearrange("e a (q r) n -> r q (e a) n", r=ROWS)
+            for r in range(ROWS):
+                load_bytes(dst[r:P:QUADRANT, :, :], rows[r])
 
-        w8v = w8_words.rearrange("(h e) a p n r -> h p (e a) (n r)", h=2)
-        w4v = w4_words.rearrange("e a p m -> a p e m")
+        def load_w8(g):
+            group = GROUPS[g]
+            load_bytes(w8[g][:], w8_words[group[0] : group[-1] + 1].rearrange("e a p n r -> p (e a) (n r)"))
 
-        for i in range(4):
+        for i, (a, first_row) in enumerate(STEPS):
             for t0, t1 in LOADS[i]:
-                load_x(i, t0, t1)
+                nc.sync.dma_start(
+                    out=raw[i, t0][:],
+                    in_=xT[a * K_PASS : (a + 1) * K_PASS, t0:t1].rearrange("(p j) w -> p j w", j=PACK),
+                )
             if i == 0:
                 nc.sync.dma_start(offs_t[:], offs)
-        for r in range(4):
-            load_scales(ws4, w4_scales, r)
-        nc.sync.dma_start(out=w4[0][:].bitcast(I32), in_=w4v[0].bitcast(I32))
-        for r in range(4):
-            load_scales(ws8, w8_scales, r)
-        for h in range(2):
-            nc.sync.dma_start(out=w8[h][:].bitcast(I32), in_=w8v[h].bitcast(I32))
-        nc.sync.dma_start(out=w4[1][:].bitcast(I32), in_=w4v[1].bitcast(I32))
+        w4_by_pass = w4_words.rearrange("e a p m -> a p e m")
+        load_planes(w4_planes, w4_scales)
+        load_bytes(w4[0][:], w4_by_pass[0])
+        load_w8(0)
+        load_planes(w8_planes, w8_scales)
+        load_w8(1)
+        load_bytes(w4[1][:], w4_by_pass[1])
+        load_w8(2)
         nc.sync.dma_start(bias[:], b)
         for r, lst in enumerate((pos1, pos2, pos3)):
             nc.sync.dma_start(pos_t[r][:], lst)
         for j in range(CHUNKS):
             nc.sync.dma_start(out=gates[j][:], in_=gate[:, :, j * CHUNK : (j + 1) * CHUNK].rearrange("r p t -> p r t"))
 
-        def multiply(i, e):
-            a, pl, k0 = PASSES[i]
-            if a < 2:
-                lhsT = w8[e // 3][:, 2 * (e % 3) + a, :].bitcast(FP8X4)
-                lhsT_scale = ws8[:, 2 * e + a, :]
+        def round_chunk(i, t0):
+            t1 = t0 + CHUNK
+            l0 = max(first for first, end in LOADS[i] if first <= t0)
+            grouped = keep.tile([P, CHUNK, PACK], BF16, name="grouped%d_%d" % (i, t0), align_bytes=64)
+            if t1 == T:
+                cut = t0 + (SHARE if i > 0 else CHUNK - SHARE)
             else:
-                lhsT = w4[a - 2][:, e, :].bitcast(FP4X4)
-                lhsT_scale = ws4[:, 2 * e + a - 2, :]
-            sl = slice(e * C, (e + 1) * C)
+                cut = t1 if i == 0 and t0 == 0 else t0
+            for on_vector, u0, u1 in ((True, t0, cut), (False, cut, t1)):
+                if u1 > u0:
+                    dst = grouped[:, u0 - t0 : u1 - t0, :].rearrange("p (c i) j -> p c j i", i=2)
+                    src = raw[i, l0][:, :, u0 - l0 : u1 - l0].rearrange("p j (c i) -> p c j i", i=2)
+                    if on_vector:
+                        nc.vector.tensor_copy(out=dst, in_=src)
+                    else:
+                        nc.scalar.activation(dst, src, COPY)
+            return grouped
+
+        def quantise(i, t0, grouped):
+            first_row = STEPS[i][1]
+            plane = lone_plane if i == 0 else shared_planes
+            nc.vector.quantize_mx(
+                out=words[i][:, t0 : t0 + CHUNK].bitcast(FP8X4),
+                scales=plane[first_row:P, t0 : t0 + CHUNK],
+                in_=grouped[:].rearrange("p w j -> p (w j)"),
+            )
+
+        def gather_words(i, s0, s1):
+            nc.vector.tensor_copy(slot_words[i][:, s0:s1], words[i][:].bitcast(U32).indirect(entries(offs_t, s0, s1)))
+
+        def multiply(i, e):
+            a, first_row = STEPS[i]
+            slots = slice(e * C, (e + 1) * C)
+            if a < FP8_PASSES:
+                g = [e in group for group in GROUPS].index(True)
+                lhsT = w8[g][:, FP8_PASSES * (e - GROUPS[g][0]) + a, :].bitcast(FP8X4)
+                lhsT_scale = w8_planes[:, 2 * e + a, :]
+            else:
+                lhsT = w4[a - FP8_PASSES][:, e, :].bitcast(FP4X4)
+                lhsT_scale = w4_planes[:, 2 * e + a - FP8_PASSES, :]
+            if i == 0:
+                rhs_scale = slot_lone[e // 2][:, (e % 2) * C : (e % 2 + 1) * C]
+            else:
+                rhs_scale = slot_shared[first_row:P, slots]
             nc.tensor.matmul_mx(
                 out=banks[e][:],
                 lhsT=lhsT,
                 lhsT_scale=lhsT_scale,
-                rhs=g_codes[i][:, sl].bitcast(FP8X4),
-                rhs_scale=g_shared[k0:P, sl] if pl == 1 else g_lone[e // 2][:, (e % 2) * C : (e % 2 + 1) * C],
+                rhs=slot_words[i][:, slots].bitcast(FP8X4),
+                rhs_scale=rhs_scale,
                 start=(i == 0),
-                stop=(i == 3),
+                stop=(i == LAST),
             )
 
-        def cast(i, on_vector, t0, t1):
-            l0 = max(a for a, z in LOADS[i] if a <= t0)
-            gr = keep.tile([P, t1 - t0, PACK], BF16, name="grouped%d_%d" % (i, t0), align_bytes=64)
-            dst = gr[:].rearrange("p (c i) t -> p c t i", i=4)
-            src = raw[i, l0][:, :, t0 - l0 : t1 - l0].rearrange("p t (c i) -> p c t i", i=4)
-            if on_vector:
-                nc.vector.tensor_copy(out=dst, in_=src)
-            else:
-                nc.scalar.activation(dst, src, COPY)
-            return gr
-
-        def quantise(i, t0, t1, gr):
-            a, pl, k0 = PASSES[i]
-            nc.vector.quantize_mx(
-                out=codes[i][:, t0:t1].bitcast(FP8X4),
-                scales=planes[pl][k0:P, t0:t1],
-                in_=gr[:].rearrange("p w j -> p (w j)"),
-            )
-
-        def gather(dst, window, s0, s1):
-            nc.vector.tensor_copy(dst[:, s0:s1], window.indirect(cols(offs_t, s0, s1)))
-
-        for i in range(4):
-            pieces = [(t0, t1, cast(i, v, t0, t1)) for v, t0, t1 in CASTS[i]]
-            for t0, t1, gr in pieces:
-                quantise(i, t0, t1, gr)
+        for i in range(len(STEPS)):
+            chunks = [(t0, round_chunk(i, t0)) for t0 in range(0, T, CHUNK)]
+            for t0, grouped in chunks:
+                quantise(i, t0, grouped)
             if i == 0:
-                gather(g_codes[i], codes[i][:].bitcast(U32), 0, S)
-            if i < 3:
-                tag = "g_lone" if i == 0 else "raw%d_%d" % (i, LOADS[i][-1][0])
-                g_lone.append(keep.tile([P, 2 * C], U8, name="g_lone%d" % i, tag=tag, align_bytes=64))
-                nc.vector.tensor_copy(g_lone[i][:], planes[0][:].indirect(cols(offs_t, 2 * C * i, 2 * C * (i + 1))))
-            if i in (1, 2):
-                gather(g_codes[i], codes[i][:].bitcast(U32), 0, S)
+                gather_words(i, 0, S)
+            if i < LAST:
+                tag = "slot_lone" if i == 0 else "raw%d_%d" % (i, LOADS[i][-1][0])
+                slot_lone.append(keep.tile([P, 2 * C], U8, name="slot_lone%d" % i, tag=tag, align_bytes=64))
+                nc.vector.tensor_copy(
+                    slot_lone[i][:], lone_plane[:].indirect(entries(offs_t, 2 * C * i, 2 * C * (i + 1)))
+                )
+            if 0 < i < LAST:
+                gather_words(i, 0, S)
         for e in range(E):
             multiply(0, e)
         for h in range(2):
-            gather(g_shared, planes[1][:], h * S // 2, (h + 1) * S // 2)
-            for e in range(3 * h, 3 * h + 3):
-                for i in (1, 2):
+            s0, s1 = h * S // 2, (h + 1) * S // 2
+            nc.vector.tensor_copy(slot_shared[:, s0:s1], shared_planes[:].indirect(entries(offs_t, s0, s1)))
+            for e in range(s0 // C, s1 // C):
+                for i in range(1, LAST):
                     multiply(i, e)
-        for group in ((0, 1, 2), (3, 4), (5,)):
-            gather(g_codes[3], codes[3][:].bitcast(U32), group[0] * C, (group[-1] + 1) * C)
+        for group in GROUPS:
+            gather_words(LAST, group[0] * C, (group[-1] + 1) * C)
             for e in group:
-                multiply(3, e)
+                multiply(LAST, e)
                 if e < E - 1:
                     nc.scalar.activation(y[:, e * C : (e + 1) * C], banks[e][:], RELU, bias=bias[:, e : e + 1])
                 else:
                     nc.vector.tensor_scalar(y[:, e * C : (e + 1) * C], banks[e][:], bias[:, e : e + 1], 0.0, ADD, MAX)
 
-        free = ["spare0", "spare1", "bank0", "bank1", "bank2", "bank3"]
+        free_banks = ["spare0", "spare1", "bank0", "bank1", "bank2", "bank3"]
+        blocks = CHUNK // P
         for j in range(CHUNKS):
             t0, t1 = j * CHUNK, (j + 1) * CHUNK
             parts = [keep.tile([P, CHUNK], F32, name="part%d_%d" % (j, r)) for r in range(TOP)]
             total = keep.tile([P, CHUNK], F32, name="total%d" % j)
             on_tensor = j < CHUNKS - 1
             if on_tensor:
-                sums = [psum.tile([P, P], F32, name="sum%d_%d" % (j, u), tag=free[3 * j + u]) for u in range(2)]
+                tags = free_banks[(blocks + 1) * j : (blocks + 1) * (j + 1)]
+                sums = [psum.tile([P, P], F32, name="sum%d_%d" % (j, u), tag=tags[u]) for u in range(blocks)]
             for r in range(TOP):
-                nc.vector.tensor_tensor(parts[r][:], y[:].indirect(cols(pos_t[r], t0, t1)), gates[j][:, r, :], MULT)
+                nc.vector.tensor_tensor(parts[r][:], y[:].indirect(entries(pos_t[r], t0, t1)), gates[j][:, r, :], MULT)
                 if on_tensor:
-                    for u in range(2):
+                    for u in range(blocks):
                         nc.tensor.matmul(
-                            sums[u][:], parts[r][:, u * P : (u + 1) * P], ident[:],
-                            start=(r == 0), stop=(r == TOP - 1), is_transpose=True,
+                            sums[u][:],
+                            parts[r][:, u * P : (u + 1) * P],
+                            ident[:],
+                            start=(r == 0),
+                            stop=(r == TOP - 1),
+                            is_transpose=True,
                         )
             if on_tensor:
-                turned = keep.tile([P, 2, P], F32, name="turned%d" % j)
-                back = psum.tile([P, CHUNK], F32, name="back%d" % j, tag=free[3 * j + 2])
-                for u in range(2):
+                turned = keep.tile([P, blocks, P], F32, name="turned%d" % j)
+                back = psum.tile([P, CHUNK], F32, name="back%d" % j, tag=tags[blocks])
+                for u in range(blocks):
                     nc.scalar.copy(turned[:, u, :], sums[u][:])
                     nc.tensor.transpose(back[:, u * P : (u + 1) * P], turned[:, u, :], ident[:])
                 nc.scalar.copy(total[:], back[:])
             else:
-                pair = keep.tile([P, CHUNK], F32, name="pair%d" % j)
+                pair = keep.tile([P, CHUNK], F32, name="pair")
                 nc.vector.tensor_tensor(pair[:], parts[0][:], parts[1][:], ADD)
                 nc.vector.tensor_tensor(total[:], pair[:], parts[2][:], ADD)
             nc.sync.dma_start(out=out[:, t0:t1], in_=total[:])

@@ -87,13 +87,13 @@ def tile_moe_ecr_lin_relu_kernel(
         nc.vector.memset(y[:, S:], 0.0)
         make_identity(nc, ident[:])
 
-        def load_bytes(dst, src):
-            nc.sync.dma_start(out=dst.bitcast(I32), in_=src.bitcast(I32))
+        def load_bytes(dst, src, queue=nc.sync):
+            queue.dma_start(out=dst.bitcast(I32), in_=src.bitcast(I32))
 
         def load_planes(dst, src):
             rows = src.rearrange("e a (q r) n -> r q (e a) n", r=ROWS)
             for r in range(ROWS):
-                load_bytes(dst[r:P:QUADRANT, :, :], rows[r])
+                load_bytes(dst[r:P:QUADRANT, :, :], rows[r], nc.gpsimd)
 
         def load_w8(g):
             group = GROUPS[g]
@@ -119,7 +119,11 @@ def tile_moe_ecr_lin_relu_kernel(
         for r, lst in enumerate((pos1, pos2, pos3)):
             nc.sync.dma_start(pos_t[r][:], lst)
         for j in range(CHUNKS):
-            nc.sync.dma_start(out=gates[j][:], in_=gate[:, :, j * CHUNK : (j + 1) * CHUNK].rearrange("r p t -> p r t"))
+            for r0, r1 in ((0, 1), (1, TOP)) if j == 0 else ((0, TOP),):
+                nc.sync.dma_start(
+                    out=gates[j][:, r0:r1, :],
+                    in_=gate[r0:r1, :, j * CHUNK : (j + 1) * CHUNK].rearrange("r p t -> p r t"),
+                )
 
         def round_chunk(i, t0):
             t1 = t0 + CHUNK

@@ -36,8 +36,9 @@ WINDOW = 1024
 
 STEPS = ((2, 0), (0, 4), (1, 8), (3, 0))
 LAST = len(STEPS) - 1
-LOADS = [[(0, 2 * CHUNK), (2 * CHUNK, T)]] + [[(t, t + CHUNK) for t in range(0, T, CHUNK)]] * LAST
-SHARE = 112
+LOADS = [[(0, 2 * CHUNK), (2 * CHUNK, T)]] * 2 + [[(t, t + CHUNK) for t in range(0, T, CHUNK)]] * 2
+SHARES = (176, 176, 128, 160)
+LONE_PARTS = ((0, 1, 2), (3,), (4,), (5,))
 GROUPS = ((0, 1, 2), (3, 4), (5,))
 
 
@@ -93,7 +94,7 @@ def tile_moe_ecr_lin_relu_kernel(
         def load_planes(dst, src):
             rows = src.rearrange("e a (q r) n -> r q (e a) n", r=ROWS)
             for r in range(ROWS):
-                load_bytes(dst[r:P:QUADRANT, :, :], rows[r], nc.gpsimd)
+                load_bytes(dst[r:P:QUADRANT, :, :], rows[r])
 
         def load_w8(g):
             group = GROUPS[g]
@@ -130,7 +131,7 @@ def tile_moe_ecr_lin_relu_kernel(
             l0 = max(first for first, end in LOADS[i] if first <= t0)
             grouped = keep.tile([P, CHUNK, PACK], BF16, name="grouped%d_%d" % (i, t0), align_bytes=64)
             if t1 == T:
-                cut = t0 + (SHARE if i > 0 else CHUNK - SHARE)
+                cut = t0 + SHARES[i]
             else:
                 cut = t1 if i == 0 and t0 == 0 else t0
             for on_vector, u0, u1 in ((True, t0, cut), (False, cut, t1)):
@@ -166,7 +167,9 @@ def tile_moe_ecr_lin_relu_kernel(
                 lhsT = w4[a - FP8_PASSES][:, e, :].bitcast(FP4X4)
                 lhsT_scale = w4_planes[:, 2 * e + a - FP8_PASSES, :]
             if i == 0:
-                rhs_scale = slot_lone[e // 2][:, (e % 2) * C : (e % 2 + 1) * C]
+                g = [e in part for part in LONE_PARTS].index(True)
+                first = e - LONE_PARTS[g][0]
+                rhs_scale = slot_lone[g][:, first * C : (first + 1) * C]
             else:
                 rhs_scale = slot_shared[first_row:P, slots]
             nc.tensor.matmul_mx(
@@ -185,11 +188,12 @@ def tile_moe_ecr_lin_relu_kernel(
                 quantise(i, t0, grouped)
             if i == 0:
                 gather_words(i, 0, S)
-            if i < LAST:
+            if True:
                 tag = "slot_lone" if i == 0 else "raw%d_%d" % (i, LOADS[i][-1][0])
-                slot_lone.append(keep.tile([P, 2 * C], U8, name="slot_lone%d" % i, tag=tag, align_bytes=64))
+                part = LONE_PARTS[i]
+                slot_lone.append(keep.tile([P, len(part) * C], U8, name="slot_lone%d" % i, tag=tag, align_bytes=64))
                 nc.vector.tensor_copy(
-                    slot_lone[i][:], lone_plane[:].indirect(entries(offs_t, 2 * C * i, 2 * C * (i + 1)))
+                    slot_lone[i][:], lone_plane[:].indirect(entries(offs_t, C * part[0], C * (part[-1] + 1)))
                 )
             if 0 < i < LAST:
                 gather_words(i, 0, S)
@@ -205,7 +209,7 @@ def tile_moe_ecr_lin_relu_kernel(
             gather_words(LAST, group[0] * C, (group[-1] + 1) * C)
             for e in group:
                 multiply(LAST, e)
-                if e < E - 1:
+                if e != E - 2:
                     nc.scalar.activation(y[:, e * C : (e + 1) * C], banks[e][:], RELU, bias=bias[:, e : e + 1])
                 else:
                     nc.vector.tensor_scalar(y[:, e * C : (e + 1) * C], banks[e][:], bias[:, e : e + 1], 0.0, ADD, MAX)

@@ -197,6 +197,17 @@ def tile_moe_ecr_lin_relu_kernel(
                 )
             if 0 < i < LAST:
                 gather_words(i, 0, S)
+        for u, width in enumerate((4 * C, 2 * C)):
+            idle = psum.tile([P, width], F32, name="idle%d" % u, tag="spare%d" % u)
+            nc.tensor.matmul_mx(
+                out=idle[:],
+                lhsT=slot_words[0][:, :C].bitcast(FP8X4),
+                lhsT_scale=w4_planes[:, 0, :],
+                rhs=slot_words[0][:, :width].bitcast(FP8X4),
+                rhs_scale=w4_planes[:, : width // C, :].rearrange("p a n -> p (a n)"),
+                start=True,
+                stop=True,
+            )
         for e in range(E):
             multiply(0, e)
         for h in range(2):

@@ -39,6 +39,7 @@ LAST = len(STEPS) - 1
 LOADS = [[(0, 2 * CHUNK), (2 * CHUNK, T)]] * 2 + [[(t, t + CHUNK) for t in range(0, T, CHUNK)]] * 2
 SHARES = (176, 176, 128, 160)
 LONE_PARTS = ((0, 1, 2), (3,), (4,), (5,))
+SPANS = ((0, 256), (256, 512), (512, 768))
 GROUPS = ((0, 1, 2), (3, 4), (5,))
 
 
@@ -77,7 +78,7 @@ def tile_moe_ecr_lin_relu_kernel(
             for i in range(len(STEPS))
             for t0, t1 in LOADS[i]
         }
-        gates = [keep.tile([P, TOP, CHUNK], F32, name="gate%d" % j) for j in range(CHUNKS)]
+        gates = [keep.tile([P, TOP, t1 - t0], F32, name="gate%d" % t0) for t0, t1 in SPANS]
 
         nc.vector.memset(w4_planes[:].rearrange("p a n -> p (a n)").bitcast(I32), 0)
         nc.vector.memset(w8_planes[:].rearrange("p a n -> p (a n)").bitcast(I32), 0)
@@ -113,17 +114,18 @@ def tile_moe_ecr_lin_relu_kernel(
         load_bytes(w4[0][:], w4_by_pass[0])
         load_w8(0)
         load_planes(w8_planes, w8_scales)
+        nc.sync.dma_start(bias[:], b)
         load_w8(1)
         load_bytes(w4[1][:], w4_by_pass[1])
         load_w8(2)
-        nc.sync.dma_start(bias[:], b)
-        for r, lst in enumerate((pos1, pos2, pos3)):
-            nc.sync.dma_start(pos_t[r][:], lst)
-        for j in range(CHUNKS):
+        for j, (t0, t1) in enumerate(SPANS):
             for r0, r1 in ((0, 1), (1, TOP)) if j == 0 else ((0, TOP),):
+                if j == 0:
+                    for r in range(r0, r1):
+                        nc.sync.dma_start(pos_t[r][:], (pos1, pos2, pos3)[r])
                 nc.sync.dma_start(
                     out=gates[j][:, r0:r1, :],
-                    in_=gate[r0:r1, :, j * CHUNK : (j + 1) * CHUNK].rearrange("r p t -> p r t"),
+                    in_=gate[r0:r1, :, t0:t1].rearrange("r p t -> p r t"),
                 )
 
         def round_chunk(i, t0):
@@ -136,8 +138,8 @@ def tile_moe_ecr_lin_relu_kernel(
                 cut = t1 if i == 0 and t0 == 0 else t0
             for on_vector, u0, u1 in ((True, t0, cut), (False, cut, t1)):
                 if u1 > u0:
-                    dst = grouped[:, u0 - t0 : u1 - t0, :].rearrange("p (c i) j -> p c j i", i=2)
-                    src = raw[i, l0][:, :, u0 - l0 : u1 - l0].rearrange("p j (c i) -> p c j i", i=2)
+                    dst = grouped[:, u0 - t0 : u1 - t0, :].rearrange("p (c i) j -> p c j i", i=4)
+                    src = raw[i, l0][:, :, u0 - l0 : u1 - l0].rearrange("p j (c i) -> p c j i", i=4)
                     if on_vector:
                         nc.vector.tensor_copy(out=dst, in_=src)
                     else:
@@ -226,17 +228,23 @@ def tile_moe_ecr_lin_relu_kernel(
                     nc.vector.tensor_scalar(y[:, e * C : (e + 1) * C], banks[e][:], bias[:, e : e + 1], 0.0, ADD, MAX)
 
         free_banks = ["spare0", "spare1", "bank0", "bank1", "bank2", "bank3"]
-        blocks = CHUNK // P
-        for j in range(CHUNKS):
-            t0, t1 = j * CHUNK, (j + 1) * CHUNK
-            parts = [keep.tile([P, CHUNK], F32, name="part%d_%d" % (j, r)) for r in range(TOP)]
-            total = keep.tile([P, CHUNK], F32, name="total%d" % j)
-            on_tensor = j < CHUNKS - 1
+        for j, (t0, t1) in enumerate(SPANS):
+            blocks = (t1 - t0) // P
+            parts = [keep.tile([P, t1 - t0], F32, name="part%d_%d" % (j, r)) for r in range(TOP)]
+            total = keep.tile([P, t1 - t0], F32, name="total%d" % j)
+            on_tensor = j < len(SPANS) - 1
             if on_tensor:
-                tags = free_banks[(blocks + 1) * j : (blocks + 1) * (j + 1)]
+                tags = ["spare0", "spare1", "bank%d" % j]
                 sums = [psum.tile([P, P], F32, name="sum%d_%d" % (j, u), tag=tags[u]) for u in range(blocks)]
             for r in range(TOP):
-                nc.vector.tensor_tensor(parts[r][:], y[:].indirect(entries(pos_t[r], t0, t1)), gates[j][:, r, :], MULT)
+                piece = t1 - t0
+                for u0 in range(0, t1 - t0, piece):
+                    nc.vector.tensor_tensor(
+                        parts[r][:, u0 : u0 + piece],
+                        y[:].indirect(entries(pos_t[r], t0 + u0, t0 + u0 + piece)),
+                        gates[j][:, r, u0 : u0 + piece],
+                        MULT,
+                    )
                 if on_tensor:
                     for u in range(blocks):
                         nc.tensor.matmul(
@@ -249,13 +257,13 @@ def tile_moe_ecr_lin_relu_kernel(
                         )
             if on_tensor:
                 turned = keep.tile([P, blocks, P], F32, name="turned%d" % j)
-                back = psum.tile([P, CHUNK], F32, name="back%d" % j, tag=tags[blocks])
+                back = psum.tile([P, t1 - t0], F32, name="back%d" % j, tag=tags[blocks])
                 for u in range(blocks):
                     nc.scalar.copy(turned[:, u, :], sums[u][:])
                     nc.tensor.transpose(back[:, u * P : (u + 1) * P], turned[:, u, :], ident[:])
                 nc.scalar.copy(total[:], back[:])
             else:
-                pair = keep.tile([P, CHUNK], F32, name="pair")
+                pair = keep.tile([P, t1 - t0], F32, name="pair")
                 nc.vector.tensor_tensor(pair[:], parts[0][:], parts[1][:], ADD)
                 nc.vector.tensor_tensor(total[:], pair[:], parts[2][:], ADD)
             nc.sync.dma_start(out=out[:, t0:t1], in_=total[:])

@@ -36,8 +36,11 @@ WINDOW = 1024
 
 STEPS = ((2, 0), (0, 4), (1, 8), (3, 0))
 LAST = len(STEPS) - 1
-LOADS = [[(0, 2 * CHUNK), (2 * CHUNK, T)]] * 2 + [[(t, t + CHUNK) for t in range(0, T, CHUNK)]] * 2
-SHARES = (176, 176, 128, 160)
+HALF = T // 2
+THIRDS = [(t, t + CHUNK) for t in range(0, T, CHUNK)]
+LOADS = [[(0, T)], [(0, HALF), (HALF, T)], [(0, HALF), (HALF, T)], THIRDS]
+QUANTS = [THIRDS, THIRDS, THIRDS, THIRDS[:2] + [(512, 640), (640, 768)]]
+SHARES = [[(0, 256), (512, 704)], [(0, 64)], [(672, 768)], [(512, 640)]]
 LONE_PARTS = ((0, 1, 2), (3,), (4,), (5,))
 SPANS = ((0, 256), (256, 512), (512, 768))
 GROUPS = ((0, 1, 2), (3, 4), (5,))
@@ -128,30 +131,25 @@ def tile_moe_ecr_lin_relu_kernel(
                     in_=gate[r0:r1, :, t0:t1].rearrange("r p t -> p r t"),
                 )
 
-        def round_chunk(i, t0):
-            t1 = t0 + CHUNK
-            l0 = max(first for first, end in LOADS[i] if first <= t0)
-            grouped = keep.tile([P, CHUNK, PACK], BF16, name="grouped%d_%d" % (i, t0), align_bytes=64)
-            if t1 == T:
-                cut = t0 + SHARES[i]
-            else:
-                cut = t1 if i == 0 and t0 == 0 else t0
-            for on_vector, u0, u1 in ((True, t0, cut), (False, cut, t1)):
-                if u1 > u0:
-                    dst = grouped[:, u0 - t0 : u1 - t0, :].rearrange("p (c i) j -> p c j i", i=4)
-                    src = raw[i, l0][:, :, u0 - l0 : u1 - l0].rearrange("p j (c i) -> p c j i", i=4)
-                    if on_vector:
-                        nc.vector.tensor_copy(out=dst, in_=src)
-                    else:
-                        nc.scalar.activation(dst, src, COPY)
+        def round_chunk(i, t0, t1):
+            grouped = keep.tile([P, t1 - t0, PACK], BF16, name="grouped%d_%d" % (i, t0), align_bytes=64)
+            cuts = sorted({t0, t1} | {t for pair in SHARES[i] + LOADS[i] for t in pair if t0 < t < t1})
+            for u0, u1 in zip(cuts, cuts[1:]):
+                l0 = max(first for first, end in LOADS[i] if first <= u0)
+                dst = grouped[:, u0 - t0 : u1 - t0, :].rearrange("p (c i) j -> p c j i", i=4)
+                src = raw[i, l0][:, :, u0 - l0 : u1 - l0].rearrange("p j (c i) -> p c j i", i=4)
+                if any(first <= u0 < end for first, end in SHARES[i]):
+                    nc.vector.tensor_copy(out=dst, in_=src)
+                else:
+                    nc.scalar.activation(dst, src, COPY)
             return grouped
 
-        def quantise(i, t0, grouped):
+        def quantise(i, t0, t1, grouped):
             first_row = STEPS[i][1]
             plane = lone_plane if i == 0 else shared_planes
             nc.vector.quantize_mx(
-                out=words[i][:, t0 : t0 + CHUNK].bitcast(FP8X4),
-                scales=plane[first_row:P, t0 : t0 + CHUNK],
+                out=words[i][:, t0:t1].bitcast(FP8X4),
+                scales=plane[first_row:P, t0:t1],
                 in_=grouped[:].rearrange("p w j -> p (w j)"),
             )
 
@@ -185,9 +183,9 @@ def tile_moe_ecr_lin_relu_kernel(
             )
 
         for i in range(len(STEPS)):
-            chunks = [(t0, round_chunk(i, t0)) for t0 in range(0, T, CHUNK)]
-            for t0, grouped in chunks:
-                quantise(i, t0, grouped)
+            chunks = [(t0, t1, round_chunk(i, t0, t1)) for t0, t1 in QUANTS[i]]
+            for t0, t1, grouped in chunks:
+                quantise(i, t0, t1, grouped)
             if i == 0:
                 gather_words(i, 0, S)
             if True:

@@ -40,7 +40,7 @@ HALF = T // 2
 THIRDS = [(t, t + CHUNK) for t in range(0, T, CHUNK)]
 LOADS = [[(0, T)], [(0, HALF), (HALF, T)], [(0, HALF), (HALF, T)], THIRDS]
 QUANTS = [THIRDS, THIRDS, THIRDS, THIRDS[:2] + [(512, 640), (640, 768)]]
-SHARES = [[(0, 256), (512, 704)], [(0, 64)], [(672, 768)], [(512, 640)]]
+SHARES = [[(0, 256), (512, 704)], [], [(672, 768)], [(512, 640)]]
 LONE_PARTS = ((0, 1, 2), (3,), (4,), (5,))
 SPANS = ((0, 256), (256, 512), (512, 768))
 GROUPS = ((0, 1, 2), (3, 4), (5,))

@@ -42,8 +42,8 @@ LOADS = [[(0, T)], [(0, HALF), (HALF, T)], [(0, HALF), (HALF, T)], THIRDS]
 QUANTS = [THIRDS, THIRDS, THIRDS, THIRDS[:2] + [(512, 640), (640, 768)]]
 SHARES = [[(0, 256), (512, 704)], [], [(672, 768)], [(512, 640)]]
 LONE_PARTS = ((0, 1, 2), (3,), (4,), (5,))
-SPANS = ((0, 256), (256, 512), (512, 768))
 GROUPS = ((0, 1, 2), (3, 4), (5,))
+EARLY, MIXED, LATE = (0, 384), (384, 512), (512, 768)
 
 
 def entries(lst, first, end):
@@ -81,7 +81,10 @@ def tile_moe_ecr_lin_relu_kernel(
             for i in range(len(STEPS))
             for t0, t1 in LOADS[i]
         }
-        gates = [keep.tile([P, TOP, t1 - t0], F32, name="gate%d" % t0) for t0, t1 in SPANS]
+        gate_loads = [(0, 1) + EARLY, (1, TOP) + EARLY, (0, 2, MIXED[0], T), (2, TOP, MIXED[0], T)]
+        gates = [
+            keep.tile([P, r1 - r0, t1 - t0], F32, name="gate%d_%d" % (r0, t0)) for r0, r1, t0, t1 in gate_loads
+        ]
 
         nc.vector.memset(w4_planes[:].rearrange("p a n -> p (a n)").bitcast(I32), 0)
         nc.vector.memset(w8_planes[:].rearrange("p a n -> p (a n)").bitcast(I32), 0)
@@ -121,15 +124,11 @@ def tile_moe_ecr_lin_relu_kernel(
         load_w8(1)
         load_bytes(w4[1][:], w4_by_pass[1])
         load_w8(2)
-        for j, (t0, t1) in enumerate(SPANS):
-            for r0, r1 in ((0, 1), (1, TOP)) if j == 0 else ((0, TOP),):
-                if j == 0:
-                    for r in range(r0, r1):
-                        nc.sync.dma_start(pos_t[r][:], (pos1, pos2, pos3)[r])
-                nc.sync.dma_start(
-                    out=gates[j][:, r0:r1, :],
-                    in_=gate[r0:r1, :, t0:t1].rearrange("r p t -> p r t"),
-                )
+        for j, (r0, r1, t0, t1) in enumerate(gate_loads):
+            if j < 2:
+                for r in range(r0, r1):
+                    nc.sync.dma_start(pos_t[r][:], (pos1, pos2, pos3)[r])
+            nc.sync.dma_start(out=gates[j][:], in_=gate[r0:r1, :, t0:t1].rearrange("r p t -> p r t"))
 
         def round_chunk(i, t0, t1):
             grouped = keep.tile([P, t1 - t0, PACK], BF16, name="grouped%d_%d" % (i, t0), align_bytes=64)
@@ -225,43 +224,49 @@ def tile_moe_ecr_lin_relu_kernel(
                 else:
                     nc.vector.tensor_scalar(y[:, e * C : (e + 1) * C], banks[e][:], bias[:, e : e + 1], 0.0, ADD, MAX)
 
-        free_banks = ["spare0", "spare1", "bank0", "bank1", "bank2", "bank3"]
-        for j, (t0, t1) in enumerate(SPANS):
+        def product(r, t0, t1):
+            j = [r0 <= r < r1 and u0 <= t0 < u1 for r0, r1, u0, u1 in gate_loads].index(True)
+            r0, r1, u0, u1 = gate_loads[j]
+            part = keep.tile([P, t1 - t0], F32, name="part%d_%d" % (r, t0))
+            nc.vector.tensor_tensor(
+                part[:], y[:].indirect(entries(pos_t[r], t0, t1)), gates[j][:, r - r0, t0 - u0 : t1 - u0], MULT
+            )
+            return part
+
+        def sum_on_tensor(lists, t0, t1, tags):
             blocks = (t1 - t0) // P
-            parts = [keep.tile([P, t1 - t0], F32, name="part%d_%d" % (j, r)) for r in range(TOP)]
-            total = keep.tile([P, t1 - t0], F32, name="total%d" % j)
-            on_tensor = j < len(SPANS) - 1
-            if on_tensor:
-                tags = ["spare0", "spare1", "bank%d" % j]
-                sums = [psum.tile([P, P], F32, name="sum%d_%d" % (j, u), tag=tags[u]) for u in range(blocks)]
-            for r in range(TOP):
-                piece = t1 - t0
-                for u0 in range(0, t1 - t0, piece):
-                    nc.vector.tensor_tensor(
-                        parts[r][:, u0 : u0 + piece],
-                        y[:].indirect(entries(pos_t[r], t0 + u0, t0 + u0 + piece)),
-                        gates[j][:, r, u0 : u0 + piece],
-                        MULT,
-                    )
-                if on_tensor:
-                    for u in range(blocks):
-                        nc.tensor.matmul(
-                            sums[u][:],
-                            parts[r][:, u * P : (u + 1) * P],
-                            ident[:],
-                            start=(r == 0),
-                            stop=(r == TOP - 1),
-                            is_transpose=True,
-                        )
-            if on_tensor:
-                turned = keep.tile([P, blocks, P], F32, name="turned%d" % j)
-                back = psum.tile([P, t1 - t0], F32, name="back%d" % j, tag=tags[blocks])
+            sums = [psum.tile([P, P], F32, name="sum%d_%d" % (t0, u), tag=tags[u]) for u in range(blocks)]
+            for r in range(lists):
+                part = product(r, t0, t1)
                 for u in range(blocks):
-                    nc.scalar.copy(turned[:, u, :], sums[u][:])
-                    nc.tensor.transpose(back[:, u * P : (u + 1) * P], turned[:, u, :], ident[:])
-                nc.scalar.copy(total[:], back[:])
-            else:
-                pair = keep.tile([P, t1 - t0], F32, name="pair")
-                nc.vector.tensor_tensor(pair[:], parts[0][:], parts[1][:], ADD)
-                nc.vector.tensor_tensor(total[:], pair[:], parts[2][:], ADD)
-            nc.sync.dma_start(out=out[:, t0:t1], in_=total[:])
+                    nc.tensor.matmul(
+                        sums[u][:],
+                        part[:, u * P : (u + 1) * P],
+                        ident[:],
+                        start=(r == 0),
+                        stop=(r == lists - 1),
+                        is_transpose=True,
+                    )
+            turned = keep.tile([P, blocks, P], F32, name="turned%d" % t0)
+            back = psum.tile([P, t1 - t0], F32, name="back%d" % t0, tag=tags[blocks])
+            for u in range(blocks):
+                nc.scalar.copy(turned[:, u, :], sums[u][:])
+                nc.tensor.transpose(back[:, u * P : (u + 1) * P], turned[:, u, :], ident[:])
+            return back
+
+        totals = {span: keep.tile([P, span[1] - span[0]], F32, name="total%d" % span[0]) for span in (EARLY, MIXED, LATE)}
+        back = sum_on_tensor(TOP, *EARLY, ["spare0", "spare1", "bank0", "bank1"])
+        nc.scalar.copy(totals[EARLY][:], back[:])
+        nc.sync.dma_start(out=out[:, EARLY[0] : EARLY[1]], in_=totals[EARLY][:])
+        back = sum_on_tensor(2, *MIXED, ["bank2", "bank3"])
+        first = product(0, *LATE)
+        pair = keep.tile([P, LATE[1] - LATE[0]], F32, name="pair")
+        halves = [(u, product(1, LATE[0] + u, LATE[0] + u + P)) for u in (0, P)]
+        for u, second in halves:
+            nc.vector.tensor_tensor(pair[:, u : u + P], first[:, u : u + P], second[:], ADD)
+        third_late = product(2, *LATE)
+        third_mixed = product(2, *MIXED)
+        nc.vector.tensor_tensor(totals[LATE][:], pair[:], third_late[:], ADD)
+        nc.sync.dma_start(out=out[:, LATE[0] : LATE[1]], in_=totals[LATE][:])
+        nc.vector.tensor_tensor(totals[MIXED][:], third_mixed[:], back[:], ADD)
+        nc.sync.dma_start(out=out[:, MIXED[0] : MIXED[1]], in_=totals[MIXED][:])

@@ -81,7 +81,7 @@ def tile_moe_ecr_lin_relu_kernel(
             for i in range(len(STEPS))
             for t0, t1 in LOADS[i]
         }
-        gate_loads = [(0, 1) + EARLY, (1, TOP) + EARLY, (0, 2, MIXED[0], T), (2, TOP, MIXED[0], T)]
+        gate_loads = [(0, 1) + EARLY, (1, TOP) + EARLY, (0, 2) + MIXED, (0, 2) + LATE, (2, TOP, MIXED[0], T)]
         gates = [
             keep.tile([P, r1 - r0, t1 - t0], F32, name="gate%d_%d" % (r0, t0)) for r0, r1, t0, t1 in gate_loads
         ]
@@ -125,9 +125,8 @@ def tile_moe_ecr_lin_relu_kernel(
         load_bytes(w4[1][:], w4_by_pass[1])
         load_w8(2)
         for j, (r0, r1, t0, t1) in enumerate(gate_loads):
-            if j < 2:
-                for r in range(r0, r1):
-                    nc.sync.dma_start(pos_t[r][:], (pos1, pos2, pos3)[r])
+            if j < TOP:
+                nc.sync.dma_start(pos_t[j][:], (pos1, pos2, pos3)[j])
             nc.sync.dma_start(out=gates[j][:], in_=gate[r0:r1, :, t0:t1].rearrange("r p t -> p r t"))
 
         def round_chunk(i, t0, t1):
@@ -237,28 +236,30 @@ def tile_moe_ecr_lin_relu_kernel(
             blocks = (t1 - t0) // P
             sums = [psum.tile([P, P], F32, name="sum%d_%d" % (t0, u), tag=tags[u]) for u in range(blocks)]
             for r in range(lists):
-                part = product(r, t0, t1)
+                by_block = r == lists - 1
+                part = None if by_block else product(r, t0, t1)
                 for u in range(blocks):
                     nc.tensor.matmul(
                         sums[u][:],
-                        part[:, u * P : (u + 1) * P],
+                        product(r, t0 + u * P, t0 + (u + 1) * P)[:] if by_block else part[:, u * P : (u + 1) * P],
                         ident[:],
                         start=(r == 0),
                         stop=(r == lists - 1),
                         is_transpose=True,
                     )
             turned = keep.tile([P, blocks, P], F32, name="turned%d" % t0)
-            back = psum.tile([P, t1 - t0], F32, name="back%d" % t0, tag=tags[blocks])
+            back = [psum.tile([P, P], F32, name="back%d_%d" % (t0, u), tag=tags[blocks + u]) for u in range(blocks)]
             for u in range(blocks):
                 nc.scalar.copy(turned[:, u, :], sums[u][:])
-                nc.tensor.transpose(back[:, u * P : (u + 1) * P], turned[:, u, :], ident[:])
+                nc.tensor.transpose(back[u][:], turned[:, u, :], ident[:])
             return back
 
         totals = {span: keep.tile([P, span[1] - span[0]], F32, name="total%d" % span[0]) for span in (EARLY, MIXED, LATE)}
-        back = sum_on_tensor(TOP, *EARLY, ["spare0", "spare1", "bank0", "bank1"])
-        nc.scalar.copy(totals[EARLY][:], back[:])
+        back = sum_on_tensor(TOP, *EARLY, ["spare0", "spare1", "bank0", "bank1", "bank2", "bank3"])
+        for u, block in enumerate(back):
+            nc.scalar.copy(totals[EARLY][:, u * P : (u + 1) * P], block[:])
         nc.sync.dma_start(out=out[:, EARLY[0] : EARLY[1]], in_=totals[EARLY][:])
-        back = sum_on_tensor(2, *MIXED, ["bank2", "bank3"])
+        back = sum_on_tensor(2, *MIXED, ["bank4", "bank5"])
         first = product(0, *LATE)
         pair = keep.tile([P, LATE[1] - LATE[0]], F32, name="pair")
         halves = [(u, product(1, LATE[0] + u, LATE[0] + u + P)) for u in (0, P)]
@@ -268,5 +269,5 @@ def tile_moe_ecr_lin_relu_kernel(
         third_mixed = product(2, *MIXED)
         nc.vector.tensor_tensor(totals[LATE][:], pair[:], third_late[:], ADD)
         nc.sync.dma_start(out=out[:, LATE[0] : LATE[1]], in_=totals[LATE][:])
-        nc.vector.tensor_tensor(totals[MIXED][:], third_mixed[:], back[:], ADD)
+        nc.vector.tensor_tensor(totals[MIXED][:], third_mixed[:], back[0][:], ADD)
         nc.sync.dma_start(out=out[:, MIXED[0] : MIXED[1]], in_=totals[MIXED][:])

@@ -40,7 +40,7 @@ HALF = T // 2
 THIRDS = [(t, t + CHUNK) for t in range(0, T, CHUNK)]
 LOADS = [[(0, T)], [(0, HALF), (HALF, T)], [(0, HALF), (HALF, T)], THIRDS]
 QUANTS = [THIRDS, THIRDS, THIRDS, THIRDS[:2] + [(512, 640), (640, 768)]]
-SHARES = [[(0, 256), (512, 704)], [], [(672, 768)], [(512, 640)]]
+SHARES = [[(0, 256), (512, 704)], [(736, 768)], [(640, 768)], [(512, 640)]]
 LONE_PARTS = ((0, 1, 2), (3,), (4,), (5,))
 GROUPS = ((0, 1, 2), (3, 4), (5,))
 EARLY, MIXED, LATE = (0, 384), (384, 512), (512, 768)

@@ -43,7 +43,7 @@ QUANTS = [THIRDS, THIRDS, THIRDS, THIRDS[:2] + [(512, 640), (640, 768)]]
 SHARES = [[(0, 256), (512, 704)], [(736, 768)], [(640, 768)], [(512, 640)]]
 LONE_PARTS = ((0, 1, 2), (3,), (4,), (5,))
 GROUPS = ((0, 1, 2), (3, 4), (5,))
-EARLY, MIXED, LATE = (0, 384), (384, 512), (512, 768)
+EARLY, LATE = (0, 512), (512, 768)
 
 
 def entries(lst, first, end):
@@ -81,10 +81,9 @@ def tile_moe_ecr_lin_relu_kernel(
             for i in range(len(STEPS))
             for t0, t1 in LOADS[i]
         }
-        gate_loads = [(0, 1) + EARLY, (1, TOP) + EARLY, (0, 2) + MIXED, (0, 2) + LATE, (2, TOP, MIXED[0], T)]
-        gates = [
-            keep.tile([P, r1 - r0, t1 - t0], F32, name="gate%d_%d" % (r0, t0)) for r0, r1, t0, t1 in gate_loads
-        ]
+        gate_loads = [(range(1, 2),) + THIRDS[0], (range(0, TOP, 2),) + THIRDS[0]]
+        gate_loads += [(range(TOP),) + third for third in THIRDS[1:]]
+        gates = [keep.tile([P, len(rs), t1 - t0], F32, name="gate%d_%d" % (rs[0], t0)) for rs, t0, t1 in gate_loads]
 
         nc.vector.memset(w4_planes[:].rearrange("p a n -> p (a n)").bitcast(I32), 0)
         nc.vector.memset(w8_planes[:].rearrange("p a n -> p (a n)").bitcast(I32), 0)
@@ -124,10 +123,11 @@ def tile_moe_ecr_lin_relu_kernel(
         load_w8(1)
         load_bytes(w4[1][:], w4_by_pass[1])
         load_w8(2)
-        for j, (r0, r1, t0, t1) in enumerate(gate_loads):
-            if j < TOP:
-                nc.sync.dma_start(pos_t[j][:], (pos1, pos2, pos3)[j])
-            nc.sync.dma_start(out=gates[j][:], in_=gate[r0:r1, :, t0:t1].rearrange("r p t -> p r t"))
+        for j, (rs, t0, t1) in enumerate(gate_loads):
+            for r in ((0, 1), (2,), (), ())[j]:
+                nc.sync.dma_start(pos_t[r][:], (pos1, pos2, pos3)[r])
+            rows = gate[rs.start : rs.stop : rs.step, :, t0:t1]
+            nc.sync.dma_start(out=gates[j][:], in_=rows.rearrange("r p t -> p r t"))
 
         def round_chunk(i, t0, t1):
             grouped = keep.tile([P, t1 - t0, PACK], BF16, name="grouped%d_%d" % (i, t0), align_bytes=64)
@@ -186,28 +186,26 @@ def tile_moe_ecr_lin_relu_kernel(
                 quantise(i, t0, t1, grouped)
             if i == 0:
                 gather_words(i, 0, S)
-            if True:
-                tag = "slot_lone" if i == 0 else "raw%d_%d" % (i, LOADS[i][-1][0])
-                part = LONE_PARTS[i]
-                slot_lone.append(keep.tile([P, len(part) * C], U8, name="slot_lone%d" % i, tag=tag, align_bytes=64))
-                nc.vector.tensor_copy(
-                    slot_lone[i][:], lone_plane[:].indirect(entries(offs_t, C * part[0], C * (part[-1] + 1)))
-                )
+            tag = "slot_lone" if i == 0 else "raw%d_%d" % (i, LOADS[i][-1][0])
+            part = LONE_PARTS[i]
+            slot_lone.append(keep.tile([P, len(part) * C], U8, name="slot_lone%d" % i, tag=tag, align_bytes=64))
+            nc.vector.tensor_copy(
+                slot_lone[i][:], lone_plane[:].indirect(entries(offs_t, C * part[0], C * (part[-1] + 1)))
+            )
             if 0 < i < LAST:
                 gather_words(i, 0, S)
-        for u, width in enumerate((4 * C, 2 * C)):
-            idle = psum.tile([P, width], F32, name="idle%d" % u, tag="spare%d" % u)
-            nc.tensor.matmul_mx(
-                out=idle[:],
-                lhsT=slot_words[0][:, :C].bitcast(FP8X4),
-                lhsT_scale=w4_planes[:, 0, :],
-                rhs=slot_words[0][:, :width].bitcast(FP8X4),
-                rhs_scale=w4_planes[:, : width // C, :].rearrange("p a n -> p (a n)"),
-                start=True,
-                stop=True,
-            )
         for e in range(E):
             multiply(0, e)
+        idle = psum.tile([P, 2 * N], F32, name="idle", tag="spare0")
+        nc.tensor.matmul_mx(
+            out=idle[:],
+            lhsT=w8[0][:, 0, :].bitcast(FP8X4),
+            lhsT_scale=w4_planes[:, 0, :],
+            rhs=w8[0][:, :2, :].rearrange("p a m -> p (a m)").bitcast(FP8X4),
+            rhs_scale=w4_planes[:, :2, :].rearrange("p a n -> p (a n)"),
+            start=True,
+            stop=True,
+        )
         for h in range(2):
             s0, s1 = h * S // 2, (h + 1) * S // 2
             nc.vector.tensor_copy(slot_shared[:, s0:s1], shared_planes[:].indirect(entries(offs_t, s0, s1)))
@@ -223,51 +221,61 @@ def tile_moe_ecr_lin_relu_kernel(
                 else:
                     nc.vector.tensor_scalar(y[:, e * C : (e + 1) * C], banks[e][:], bias[:, e : e + 1], 0.0, ADD, MAX)
 
+        def gate_of(r, t0, t1):
+            j = [r in rs and u0 <= t0 < u1 for rs, u0, u1 in gate_loads].index(True)
+            rs, u0, u1 = gate_loads[j]
+            return gates[j][:, list(rs).index(r), t0 - u0 : t1 - u0]
+
         def product(r, t0, t1):
-            j = [r0 <= r < r1 and u0 <= t0 < u1 for r0, r1, u0, u1 in gate_loads].index(True)
-            r0, r1, u0, u1 = gate_loads[j]
             part = keep.tile([P, t1 - t0], F32, name="part%d_%d" % (r, t0))
-            nc.vector.tensor_tensor(
-                part[:], y[:].indirect(entries(pos_t[r], t0, t1)), gates[j][:, r - r0, t0 - u0 : t1 - u0], MULT
-            )
+            if r == 0:
+                results = fetched[t0, t1][:]
+            else:
+                results = y[:].indirect(entries(pos_t[r], t0, t1))
+            nc.vector.tensor_tensor(part[:], results, gate_of(r, t0, t1), MULT)
             return part
 
-        def sum_on_tensor(lists, t0, t1, tags):
-            blocks = (t1 - t0) // P
-            sums = [psum.tile([P, P], F32, name="sum%d_%d" % (t0, u), tag=tags[u]) for u in range(blocks)]
-            for r in range(lists):
-                by_block = r == lists - 1
-                part = None if by_block else product(r, t0, t1)
-                for u in range(blocks):
-                    nc.tensor.matmul(
-                        sums[u][:],
-                        product(r, t0 + u * P, t0 + (u + 1) * P)[:] if by_block else part[:, u * P : (u + 1) * P],
-                        ident[:],
-                        start=(r == 0),
-                        stop=(r == lists - 1),
-                        is_transpose=True,
-                    )
-            turned = keep.tile([P, blocks, P], F32, name="turned%d" % t0)
-            back = [psum.tile([P, P], F32, name="back%d_%d" % (t0, u), tag=tags[blocks + u]) for u in range(blocks)]
-            for u in range(blocks):
-                nc.scalar.copy(turned[:, u, :], sums[u][:])
-                nc.tensor.transpose(back[u][:], turned[:, u, :], ident[:])
-            return back
+        fetched = {}
+        for t0, t1 in THIRDS:
+            fetched[t0, t1] = keep.tile([P, t1 - t0], F32, name="fetched%d" % t0)
+            nc.scalar.activation(fetched[t0, t1][:], y[:].indirect(entries(pos_t[0], t0, t1)), COPY)
 
-        totals = {span: keep.tile([P, span[1] - span[0]], F32, name="total%d" % span[0]) for span in (EARLY, MIXED, LATE)}
-        back = sum_on_tensor(TOP, *EARLY, ["spare0", "spare1", "bank0", "bank1", "bank2", "bank3"])
-        for u, block in enumerate(back):
-            nc.scalar.copy(totals[EARLY][:, u * P : (u + 1) * P], block[:])
-        nc.sync.dma_start(out=out[:, EARLY[0] : EARLY[1]], in_=totals[EARLY][:])
-        back = sum_on_tensor(2, *MIXED, ["bank4", "bank5"])
+        pairs = [(t, t + 2 * P) for t in range(EARLY[0], EARLY[1], 2 * P)]
+        sums = [psum.tile([P, 2, P], F32, name="sum%d" % h, tag="bank%d" % h) for h in range(len(pairs))]
+
+        def turn(h, part, start, stop):
+            for u in range(2):
+                nc.tensor.matmul(
+                    sums[h][:, u, :],
+                    part[:, u * P : (u + 1) * P],
+                    ident[:],
+                    start=start and u == 0,
+                    stop=stop and u == 1,
+                    is_transpose=True,
+                )
+
+        for h, (t0, t1) in enumerate(pairs):
+            for r in (1, 2, 0):
+                turn(h, product(r, t0, t1), r == 1, r == 0)
+        backs = []
+        for h in range(len(pairs)):
+            turned = keep.tile([P, 2, P], F32, name="turned%d" % h)
+            nc.scalar.copy(turned[:], sums[h][:])
+            backs.append(psum.tile([P, 2, P], F32, name="back%d" % h, tag="spare%d" % h))
+            for u in range(2):
+                nc.tensor.transpose(backs[h][:, u, :], turned[:, u, :], ident[:])
+        for h, (t0, t1) in enumerate(pairs):
+            total = keep.tile([P, 2, P], F32, name="total%d" % h)
+            nc.scalar.copy(total[:], backs[h][:])
+            nc.sync.dma_start(out=out[:, t0:t1], in_=total[:].rearrange("p u t -> p (u t)"))
+
+        second = product(1, *LATE)
         first = product(0, *LATE)
         pair = keep.tile([P, LATE[1] - LATE[0]], F32, name="pair")
-        halves = [(u, product(1, LATE[0] + u, LATE[0] + u + P)) for u in (0, P)]
-        for u, second in halves:
-            nc.vector.tensor_tensor(pair[:, u : u + P], first[:, u : u + P], second[:], ADD)
-        third_late = product(2, *LATE)
-        third_mixed = product(2, *MIXED)
-        nc.vector.tensor_tensor(totals[LATE][:], pair[:], third_late[:], ADD)
-        nc.sync.dma_start(out=out[:, LATE[0] : LATE[1]], in_=totals[LATE][:])
-        nc.vector.tensor_tensor(totals[MIXED][:], third_mixed[:], back[0][:], ADD)
-        nc.sync.dma_start(out=out[:, MIXED[0] : MIXED[1]], in_=totals[MIXED][:])
+        late_total = keep.tile([P, LATE[1] - LATE[0]], F32, name="late_total")
+        third = [product(2, LATE[0], LATE[0] + P)]
+        nc.vector.tensor_tensor(pair[:], first[:], second[:], ADD)
+        third.append(product(2, LATE[0] + P, LATE[1]))
+        for u in range(2):
+            nc.vector.tensor_tensor(late_total[:, u * P : (u + 1) * P], pair[:, u * P : (u + 1) * P], third[u][:], ADD)
+        nc.sync.dma_start(out=out[:, LATE[0] : LATE[1]], in_=late_total[:])

@@ -43,7 +43,7 @@ QUANTS = [THIRDS, THIRDS, THIRDS, THIRDS[:2] + [(512, 640), (640, 768)]]
 SHARES = [[(0, 256), (512, 704)], [(736, 768)], [(640, 768)], [(512, 640)]]
 LONE_PARTS = ((0, 1, 2), (3,), (4,), (5,))
 GROUPS = ((0, 1, 2), (3, 4), (5,))
-EARLY, LATE = (0, 512), (512, 768)
+BLOCKS = T // P
 
 
 def entries(lst, first, end):
@@ -81,9 +81,8 @@ def tile_moe_ecr_lin_relu_kernel(
             for i in range(len(STEPS))
             for t0, t1 in LOADS[i]
         }
-        gate_loads = [(range(1, 2),) + THIRDS[0], (range(0, TOP, 2),) + THIRDS[0]]
-        gate_loads += [(range(TOP),) + third for third in THIRDS[1:]]
-        gates = [keep.tile([P, len(rs), t1 - t0], F32, name="gate%d_%d" % (rs[0], t0)) for rs, t0, t1 in gate_loads]
+        gates = {r: keep.tile([P, T], F32, name="gate%d" % r) for r in (1, 2)}
+        turned_gate = keep.tile([P, BLOCKS], F32, name="turned_gate")
 
         nc.vector.memset(w4_planes[:].rearrange("p a n -> p (a n)").bitcast(I32), 0)
         nc.vector.memset(w8_planes[:].rearrange("p a n -> p (a n)").bitcast(I32), 0)
@@ -123,11 +122,13 @@ def tile_moe_ecr_lin_relu_kernel(
         load_w8(1)
         load_bytes(w4[1][:], w4_by_pass[1])
         load_w8(2)
-        for j, (rs, t0, t1) in enumerate(gate_loads):
-            for r in ((0, 1), (2,), (), ())[j]:
-                nc.sync.dma_start(pos_t[r][:], (pos1, pos2, pos3)[r])
-            rows = gate[rs.start : rs.stop : rs.step, :, t0:t1]
-            nc.sync.dma_start(out=gates[j][:], in_=rows.rearrange("r p t -> p r t"))
+        nc.sync.dma_start(pos_t[0][:], pos1)
+        nc.sync.dma_start(pos_t[1][:], pos2)
+        nc.sync.dma_start(gates[1][:], gate[1])
+        nc.sync.dma_start(pos_t[2][:], pos3)
+        with nc.allow_non_contiguous_dma(reason="one gate a partition and block"):
+            nc.sync.dma_start(turned_gate[:], gate[0, 0, :].rearrange("(u p) -> p u", p=P))
+        nc.sync.dma_start(gates[2][:], gate[2])
 
         def round_chunk(i, t0, t1):
             grouped = keep.tile([P, t1 - t0, PACK], BF16, name="grouped%d_%d" % (i, t0), align_bytes=64)
@@ -221,61 +222,34 @@ def tile_moe_ecr_lin_relu_kernel(
                 else:
                     nc.vector.tensor_scalar(y[:, e * C : (e + 1) * C], banks[e][:], bias[:, e : e + 1], 0.0, ADD, MAX)
 
-        def gate_of(r, t0, t1):
-            j = [r in rs and u0 <= t0 < u1 for rs, u0, u1 in gate_loads].index(True)
-            rs, u0, u1 = gate_loads[j]
-            return gates[j][:, list(rs).index(r), t0 - u0 : t1 - u0]
-
         def product(r, t0, t1):
             part = keep.tile([P, t1 - t0], F32, name="part%d_%d" % (r, t0))
-            if r == 0:
-                results = fetched[t0, t1][:]
-            else:
-                results = y[:].indirect(entries(pos_t[r], t0, t1))
-            nc.vector.tensor_tensor(part[:], results, gate_of(r, t0, t1), MULT)
+            nc.vector.tensor_tensor(part[:], y[:].indirect(entries(pos_t[r], t0, t1)), gates[r][:, t0:t1], MULT)
             return part
 
-        fetched = {}
-        for t0, t1 in THIRDS:
-            fetched[t0, t1] = keep.tile([P, t1 - t0], F32, name="fetched%d" % t0)
-            nc.scalar.activation(fetched[t0, t1][:], y[:].indirect(entries(pos_t[0], t0, t1)), COPY)
-
-        pairs = [(t, t + 2 * P) for t in range(EARLY[0], EARLY[1], 2 * P)]
-        sums = [psum.tile([P, 2, P], F32, name="sum%d" % h, tag="bank%d" % h) for h in range(len(pairs))]
-
-        def turn(h, part, start, stop):
+        turned = []
+        for h, (t0, t1) in enumerate(THIRDS):
+            fetched = keep.tile([P, CHUNK], F32, name="fetched%d" % h)
+            nc.scalar.activation(fetched[:], y[:].indirect(entries(pos_t[0], t0, t1)), COPY)
+            turned.append(psum.tile([P, 2, P], F32, name="turned%d" % h, tag="bank%d" % h))
             for u in range(2):
-                nc.tensor.matmul(
-                    sums[h][:, u, :],
-                    part[:, u * P : (u + 1) * P],
-                    ident[:],
-                    start=start and u == 0,
-                    stop=stop and u == 1,
-                    is_transpose=True,
-                )
-
-        for h, (t0, t1) in enumerate(pairs):
-            for r in (1, 2, 0):
-                turn(h, product(r, t0, t1), r == 1, r == 0)
+                nc.tensor.transpose(turned[h][:, u, :], fetched[:, u * P : (u + 1) * P], ident[:])
         backs = []
-        for h in range(len(pairs)):
-            turned = keep.tile([P, 2, P], F32, name="turned%d" % h)
-            nc.scalar.copy(turned[:], sums[h][:])
-            backs.append(psum.tile([P, 2, P], F32, name="back%d" % h, tag="spare%d" % h))
+        for h in range(CHUNKS):
+            scaled = keep.tile([P, 2, P], F32, name="scaled%d" % h)
+            backs.append(psum.tile([P, 2, P], F32, name="back%d" % h, tag="bank%d" % (CHUNKS + h)))
             for u in range(2):
-                nc.tensor.transpose(backs[h][:, u, :], turned[:, u, :], ident[:])
-        for h, (t0, t1) in enumerate(pairs):
-            total = keep.tile([P, 2, P], F32, name="total%d" % h)
-            nc.scalar.copy(total[:], backs[h][:])
-            nc.sync.dma_start(out=out[:, t0:t1], in_=total[:].rearrange("p u t -> p (u t)"))
+                column = turned_gate[:, 2 * h + u : 2 * h + u + 1]
+                nc.scalar.activation(scaled[:, u, :], turned[h][:, u, :], COPY, scale=column)
+                nc.tensor.transpose(backs[h][:, u, :], scaled[:, u, :], ident[:])
 
-        second = product(1, *LATE)
-        first = product(0, *LATE)
-        pair = keep.tile([P, LATE[1] - LATE[0]], F32, name="pair")
-        late_total = keep.tile([P, LATE[1] - LATE[0]], F32, name="late_total")
-        third = [product(2, LATE[0], LATE[0] + P)]
-        nc.vector.tensor_tensor(pair[:], first[:], second[:], ADD)
-        third.append(product(2, LATE[0] + P, LATE[1]))
-        for u in range(2):
-            nc.vector.tensor_tensor(late_total[:, u * P : (u + 1) * P], pair[:, u * P : (u + 1) * P], third[u][:], ADD)
-        nc.sync.dma_start(out=out[:, LATE[0] : LATE[1]], in_=late_total[:])
+        spans = ((0, 2 * CHUNK), (2 * CHUNK, T))
+        second = product(1, 0, T)
+        third = [product(2, t0, t1) for t0, t1 in spans]
+        pair = keep.tile([P, T], F32, name="pair")
+        for (t0, t1), part in zip(spans, third):
+            nc.vector.tensor_tensor(pair[:, t0:t1], second[:, t0:t1], part[:], ADD)
+        for h, (t0, t1) in enumerate(THIRDS):
+            total = keep.tile([P, CHUNK], F32, name="total%d" % h)
+            nc.vector.tensor_tensor(total[:], pair[:, t0:t1], backs[h][:].rearrange("p u t -> p (u t)"), ADD)
+            nc.sync.dma_start(out=out[:, t0:t1], in_=total[:])

@@ -81,7 +81,9 @@ def tile_moe_ecr_lin_relu_kernel(
             for i in range(len(STEPS))
             for t0, t1 in LOADS[i]
         }
-        gates = {r: keep.tile([P, T], F32, name="gate%d" % r) for r in (1, 2)}
+        gate_loads = ((1, 0, CHUNK), (1, CHUNK, T), (2, 0, T))
+        gates = [keep.tile([P, t1 - t0], F32, name="gate%d_%d" % (r, t0)) for r, t0, t1 in gate_loads]
+        gate_rows = keep.tile([P, P], F32, name="gate_rows")
         turned_gate = keep.tile([P, BLOCKS], F32, name="turned_gate")
 
         nc.vector.memset(w4_planes[:].rearrange("p a n -> p (a n)").bitcast(I32), 0)
@@ -91,6 +93,7 @@ def tile_moe_ecr_lin_relu_kernel(
         for step_words in words:
             nc.vector.memset(step_words[:, T:], 0)
         nc.vector.memset(y[:, S:], 0.0)
+        nc.vector.memset(gate_rows[:], 0.0)
         make_identity(nc, ident[:])
 
         def load_bytes(dst, src, queue=nc.sync):
@@ -113,6 +116,7 @@ def tile_moe_ecr_lin_relu_kernel(
                 )
             if i == 0:
                 nc.sync.dma_start(offs_t[:], offs)
+        nc.sync.dma_start(gate_rows[:BLOCKS, :], gate[0, 0, :].rearrange("(u t) -> u t", t=P))
         w4_by_pass = w4_words.rearrange("e a p m -> a p e m")
         load_planes(w4_planes, w4_scales)
         load_bytes(w4[0][:], w4_by_pass[0])
@@ -124,11 +128,12 @@ def tile_moe_ecr_lin_relu_kernel(
         load_w8(2)
         nc.sync.dma_start(pos_t[0][:], pos1)
         nc.sync.dma_start(pos_t[1][:], pos2)
-        nc.sync.dma_start(gates[1][:], gate[1])
-        nc.sync.dma_start(pos_t[2][:], pos3)
-        with nc.allow_non_contiguous_dma(reason="one gate a partition and block"):
-            nc.sync.dma_start(turned_gate[:], gate[0, 0, :].rearrange("(u p) -> p u", p=P))
-        nc.sync.dma_start(gates[2][:], gate[2])
+        for tile, (r, t0, t1) in zip(gates, gate_loads):
+            if r == 2:
+                nc.sync.dma_start(pos_t[2][:], pos3)
+            nc.sync.dma_start(tile[:], gate[r, :, t0:t1])
+        gate_bank = psum.tile([P, P], F32, name="gate_bank", tag="spare1")
+        nc.tensor.transpose(gate_bank[:], gate_rows[:], ident[:])
 
         def round_chunk(i, t0, t1):
             grouped = keep.tile([P, t1 - t0, PACK], BF16, name="grouped%d_%d" % (i, t0), align_bytes=64)
@@ -195,6 +200,7 @@ def tile_moe_ecr_lin_relu_kernel(
             )
             if 0 < i < LAST:
                 gather_words(i, 0, S)
+        nc.scalar.copy(turned_gate[:], gate_bank[:, :BLOCKS])
         for e in range(E):
             multiply(0, e)
         idle = psum.tile([P, 2 * N], F32, name="idle", tag="spare0")
@@ -222,10 +228,10 @@ def tile_moe_ecr_lin_relu_kernel(
                 else:
                     nc.vector.tensor_scalar(y[:, e * C : (e + 1) * C], banks[e][:], bias[:, e : e + 1], 0.0, ADD, MAX)
 
-        def product(r, t0, t1):
-            part = keep.tile([P, t1 - t0], F32, name="part%d_%d" % (r, t0))
-            nc.vector.tensor_tensor(part[:], y[:].indirect(entries(pos_t[r], t0, t1)), gates[r][:, t0:t1], MULT)
-            return part
+        def product(r, t0, t1, part):
+            j = [r == q and u0 <= t0 < u1 for q, u0, u1 in gate_loads].index(True)
+            weights = gates[j][:, t0 - gate_loads[j][1] : t1 - gate_loads[j][1]]
+            nc.vector.tensor_tensor(part, y[:].indirect(entries(pos_t[r], t0, t1)), weights, MULT)
 
         turned = []
         for h, (t0, t1) in enumerate(THIRDS):
@@ -244,11 +250,15 @@ def tile_moe_ecr_lin_relu_kernel(
                 nc.tensor.transpose(backs[h][:, u, :], scaled[:, u, :], ident[:])
 
         spans = ((0, 2 * CHUNK), (2 * CHUNK, T))
-        second = product(1, 0, T)
-        third = [product(2, t0, t1) for t0, t1 in spans]
+        second = keep.tile([P, T], F32, name="second")
+        third = keep.tile([P, T], F32, name="third")
         pair = keep.tile([P, T], F32, name="pair")
-        for (t0, t1), part in zip(spans, third):
-            nc.vector.tensor_tensor(pair[:, t0:t1], second[:, t0:t1], part[:], ADD)
+        for r, t0, t1 in gate_loads[:2]:
+            product(r, t0, t1, second[:, t0:t1])
+        for t0, t1 in spans:
+            product(2, t0, t1, third[:, t0:t1])
+        for t0, t1 in spans:
+            nc.vector.tensor_tensor(pair[:, t0:t1], second[:, t0:t1], third[:, t0:t1], ADD)
         for h, (t0, t1) in enumerate(THIRDS):
             total = keep.tile([P, CHUNK], F32, name="total%d" % h)
             nc.vector.tensor_tensor(total[:], pair[:, t0:t1], backs[h][:].rearrange("p u t -> p (u t)"), ADD)

@@ -38,7 +38,8 @@ STEPS = ((2, 0), (0, 4), (1, 8), (3, 0))
 LAST = len(STEPS) - 1
 HALF = T // 2
 THIRDS = [(t, t + CHUNK) for t in range(0, T, CHUNK)]
-LOADS = [[(0, T)], [(0, HALF), (HALF, T)], [(0, HALF), (HALF, T)], THIRDS]
+HALVES = [(0, HALF), (HALF, T)]
+LOADS = [[(0, T)], HALVES, HALVES, THIRDS]
 QUANTS = [THIRDS, THIRDS, THIRDS, THIRDS[:2] + [(512, 640), (640, 768)]]
 SHARES = [[(0, 256), (512, 704)], [(736, 768)], [(640, 768)], [(512, 640)]]
 LONE_PARTS = ((0, 1, 2), (3,), (4,), (5,))
@@ -81,7 +82,7 @@ def tile_moe_ecr_lin_relu_kernel(
             for i in range(len(STEPS))
             for t0, t1 in LOADS[i]
         }
-        gate_loads = ((1, 0, CHUNK), (1, CHUNK, T), (2, 0, T))
+        gate_loads = ((1, 0, HALF), (2, 0, T), (1, HALF, T))
         gates = [keep.tile([P, t1 - t0], F32, name="gate%d_%d" % (r, t0)) for r, t0, t1 in gate_loads]
         gate_rows = keep.tile([P, P], F32, name="gate_rows")
         turned_gate = keep.tile([P, BLOCKS], F32, name="turned_gate")
@@ -234,32 +235,29 @@ def tile_moe_ecr_lin_relu_kernel(
             nc.vector.tensor_tensor(part, y[:].indirect(entries(pos_t[r], t0, t1)), weights, MULT)
 
         turned = []
-        for h, (t0, t1) in enumerate(THIRDS):
-            fetched = keep.tile([P, CHUNK], F32, name="fetched%d" % h)
-            nc.scalar.activation(fetched[:], y[:].indirect(entries(pos_t[0], t0, t1)), COPY)
-            turned.append(psum.tile([P, 2, P], F32, name="turned%d" % h, tag="bank%d" % h))
-            for u in range(2):
-                nc.tensor.transpose(turned[h][:, u, :], fetched[:, u * P : (u + 1) * P], ident[:])
+        for h, t0 in enumerate((0, HALF)):
+            fetched = keep.tile([P, HALF], F32, name="fetched%d" % h)
+            nc.scalar.activation(fetched[:], y[:].indirect(entries(pos_t[0], t0, t0 + HALF)), COPY)
+            turned.append(psum.tile([P, HALF], F32, name="turned%d" % h, tag="bank%d" % h))
+            for u in range(0, HALF, P):
+                nc.tensor.transpose(turned[h][:, u : u + P], fetched[:, u : u + P], ident[:])
         backs = []
-        for h in range(CHUNKS):
-            scaled = keep.tile([P, 2, P], F32, name="scaled%d" % h)
-            backs.append(psum.tile([P, 2, P], F32, name="back%d" % h, tag="bank%d" % (CHUNKS + h)))
-            for u in range(2):
-                column = turned_gate[:, 2 * h + u : 2 * h + u + 1]
-                nc.scalar.activation(scaled[:, u, :], turned[h][:, u, :], COPY, scale=column)
-                nc.tensor.transpose(backs[h][:, u, :], scaled[:, u, :], ident[:])
+        for h, (t0, t1) in enumerate(HALVES):
+            scaled = keep.tile([P, t1 - t0], F32, name="scaled%d" % h)
+            backs.append(psum.tile([P, t1 - t0], F32, name="back%d" % h, tag="bank%d" % (2 + h)))
+            for t in range(t0, t1, P):
+                block = slice(t - t0, t - t0 + P)
+                source = turned[t // HALF][:, t % HALF : t % HALF + P]
+                nc.scalar.activation(scaled[:, block], source, COPY, scale=turned_gate[:, t // P : t // P + 1])
+                nc.tensor.transpose(backs[h][:, block], scaled[:, block], ident[:])
 
-        spans = ((0, 2 * CHUNK), (2 * CHUNK, T))
-        second = keep.tile([P, T], F32, name="second")
-        third = keep.tile([P, T], F32, name="third")
+        parts = [keep.tile([P, t1 - t0], F32, name="part%d_%d" % (r, t0)) for r, t0, t1 in gate_loads]
+        for part, (r, t0, t1) in zip(parts, gate_loads):
+            product(r, t0, t1, part[:])
         pair = keep.tile([P, T], F32, name="pair")
-        for r, t0, t1 in gate_loads[:2]:
-            product(r, t0, t1, second[:, t0:t1])
-        for t0, t1 in spans:
-            product(2, t0, t1, third[:, t0:t1])
-        for t0, t1 in spans:
-            nc.vector.tensor_tensor(pair[:, t0:t1], second[:, t0:t1], third[:, t0:t1], ADD)
-        for h, (t0, t1) in enumerate(THIRDS):
-            total = keep.tile([P, CHUNK], F32, name="total%d" % h)
-            nc.vector.tensor_tensor(total[:], pair[:, t0:t1], backs[h][:].rearrange("p u t -> p (u t)"), ADD)
+        for t0, second in ((0, parts[0]), (HALF, parts[2])):
+            nc.vector.tensor_tensor(pair[:, t0 : t0 + HALF], second[:], parts[1][:, t0 : t0 + HALF], ADD)
+        for h, (t0, t1) in enumerate(HALVES):
+            total = keep.tile([P, t1 - t0], F32, name="total%d" % h)
+            nc.vector.tensor_tensor(total[:], pair[:, t0:t1], backs[h][:], ADD)
             nc.sync.dma_start(out=out[:, t0:t1], in_=total[:])

@@ -82,7 +82,7 @@ def tile_moe_ecr_lin_relu_kernel(
             for i in range(len(STEPS))
             for t0, t1 in LOADS[i]
         }
-        gate_loads = ((1, 0, HALF), (2, 0, T), (1, HALF, T))
+        gate_loads = ((1, 0, HALF), (1, HALF, T), (2, 0, T))
         gates = [keep.tile([P, t1 - t0], F32, name="gate%d_%d" % (r, t0)) for r, t0, t1 in gate_loads]
         gate_rows = keep.tile([P, P], F32, name="gate_rows")
         turned_gate = keep.tile([P, BLOCKS], F32, name="turned_gate")
@@ -235,28 +235,30 @@ def tile_moe_ecr_lin_relu_kernel(
             nc.vector.tensor_tensor(part, y[:].indirect(entries(pos_t[r], t0, t1)), weights, MULT)
 
         turned = []
-        for h, t0 in enumerate((0, HALF)):
-            fetched = keep.tile([P, HALF], F32, name="fetched%d" % h)
-            nc.scalar.activation(fetched[:], y[:].indirect(entries(pos_t[0], t0, t0 + HALF)), COPY)
-            turned.append(psum.tile([P, HALF], F32, name="turned%d" % h, tag="bank%d" % h))
-            for u in range(0, HALF, P):
+        for h, (t0, t1) in enumerate(THIRDS):
+            fetched = keep.tile([P, CHUNK], F32, name="fetched%d" % h)
+            nc.scalar.activation(fetched[:], y[:].indirect(entries(pos_t[0], t0, t1)), COPY)
+            turned.append(psum.tile([P, CHUNK], F32, name="turned%d" % h, tag="bank%d" % h))
+            for u in range(0, CHUNK, P):
                 nc.tensor.transpose(turned[h][:, u : u + P], fetched[:, u : u + P], ident[:])
         backs = []
         for h, (t0, t1) in enumerate(HALVES):
             scaled = keep.tile([P, t1 - t0], F32, name="scaled%d" % h)
-            backs.append(psum.tile([P, t1 - t0], F32, name="back%d" % h, tag="bank%d" % (2 + h)))
+            backs.append(psum.tile([P, t1 - t0], F32, name="back%d" % h, tag="bank%d" % (CHUNKS + h)))
             for t in range(t0, t1, P):
                 block = slice(t - t0, t - t0 + P)
-                source = turned[t // HALF][:, t % HALF : t % HALF + P]
+                source = turned[t // CHUNK][:, t % CHUNK : t % CHUNK + P]
                 nc.scalar.activation(scaled[:, block], source, COPY, scale=turned_gate[:, t // P : t // P + 1])
                 nc.tensor.transpose(backs[h][:, block], scaled[:, block], ident[:])
 
-        parts = [keep.tile([P, t1 - t0], F32, name="part%d_%d" % (r, t0)) for r, t0, t1 in gate_loads]
-        for part, (r, t0, t1) in zip(parts, gate_loads):
-            product(r, t0, t1, part[:])
+        parts = {}
+        for r in (1, 2):
+            for t0, t1 in HALVES:
+                parts[r, t0] = keep.tile([P, HALF], F32, name="part%d_%d" % (r, t0))
+                product(r, t0, t1, parts[r, t0][:])
         pair = keep.tile([P, T], F32, name="pair")
-        for t0, second in ((0, parts[0]), (HALF, parts[2])):
-            nc.vector.tensor_tensor(pair[:, t0 : t0 + HALF], second[:], parts[1][:, t0 : t0 + HALF], ADD)
+        for t0, t1 in HALVES:
+            nc.vector.tensor_tensor(pair[:, t0:t1], parts[1, t0][:], parts[2, t0][:], ADD)
         for h, (t0, t1) in enumerate(HALVES):
             total = keep.tile([P, t1 - t0], F32, name="total%d" % h)
             nc.vector.tensor_tensor(total[:], pair[:, t0:t1], backs[h][:], ADD)

@@ -39,9 +39,10 @@ LAST = len(STEPS) - 1
 HALF = T // 2
 THIRDS = [(t, t + CHUNK) for t in range(0, T, CHUNK)]
 HALVES = [(0, HALF), (HALF, T)]
-LOADS = [[(0, T)], HALVES, HALVES, THIRDS]
+LOADS = [[(0, T)], [(0, T)], HALVES, THIRDS]
+ROW_CUTS = [((0, 2), (2, PACK))] + [((0, PACK),)] * LAST
 QUANTS = [THIRDS, THIRDS, THIRDS, THIRDS[:2] + [(512, 640), (640, 768)]]
-SHARES = [[(0, 256), (512, 704)], [(736, 768)], [(640, 768)], [(512, 640)]]
+SHARES = [[(0, 448)], [(512, 768)], [(736, 768)], [(512, 640)]]
 LONE_PARTS = ((0, 1, 2), (3,), (4,), (5,))
 GROUPS = ((0, 1, 2), (3, 4), (5,))
 BLOCKS = T // P
@@ -76,11 +77,16 @@ def tile_moe_ecr_lin_relu_kernel(
         ident = keep.tile([P, P], F32, name="ident")
         banks = [psum.tile([P, C], F32, name="bank%d" % e, tag="bank%d" % e) for e in range(E)]
         raw = {
-            (i, t0): keep.tile(
-                [P, PACK, t1 - t0], F32, name="raw%d_%d" % (i, t0), tag="raw%d_%d" % (i, t0), align_bytes=64
+            (i, t0, j0): keep.tile(
+                [P, j1 - j0, t1 - t0],
+                F32,
+                name="raw%d_%d_%d" % (i, t0, j0),
+                tag="raw%d_%d_%d" % (i, t0, j0),
+                align_bytes=64,
             )
             for i in range(len(STEPS))
             for t0, t1 in LOADS[i]
+            for j0, j1 in ROW_CUTS[i]
         }
         gate_loads = ((1, 0, HALF), (1, HALF, T), (2, 0, T))
         gates = [keep.tile([P, t1 - t0], F32, name="gate%d_%d" % (r, t0)) for r, t0, t1 in gate_loads]
@@ -111,10 +117,9 @@ def tile_moe_ecr_lin_relu_kernel(
 
         for i, (a, first_row) in enumerate(STEPS):
             for t0, t1 in LOADS[i]:
-                nc.sync.dma_start(
-                    out=raw[i, t0][:],
-                    in_=xT[a * K_PASS : (a + 1) * K_PASS, t0:t1].rearrange("(p j) w -> p j w", j=PACK),
-                )
+                rows = xT[a * K_PASS : (a + 1) * K_PASS, t0:t1].rearrange("(p j) w -> p j w", j=PACK)
+                for j0, j1 in ROW_CUTS[i]:
+                    nc.sync.dma_start(out=raw[i, t0, j0][:], in_=rows[:, j0:j1, :])
             if i == 0:
                 nc.sync.dma_start(offs_t[:], offs)
         nc.sync.dma_start(gate_rows[:BLOCKS, :], gate[0, 0, :].rearrange("(u t) -> u t", t=P))
@@ -136,18 +141,16 @@ def tile_moe_ecr_lin_relu_kernel(
         gate_bank = psum.tile([P, P], F32, name="gate_bank", tag="spare1")
         nc.tensor.transpose(gate_bank[:], gate_rows[:], ident[:])
 
-        def round_chunk(i, t0, t1):
-            grouped = keep.tile([P, t1 - t0, PACK], BF16, name="grouped%d_%d" % (i, t0), align_bytes=64)
+        def round_chunk(i, t0, t1, j0, j1, grouped):
             cuts = sorted({t0, t1} | {t for pair in SHARES[i] + LOADS[i] for t in pair if t0 < t < t1})
             for u0, u1 in zip(cuts, cuts[1:]):
                 l0 = max(first for first, end in LOADS[i] if first <= u0)
-                dst = grouped[:, u0 - t0 : u1 - t0, :].rearrange("p (c i) j -> p c j i", i=4)
-                src = raw[i, l0][:, :, u0 - l0 : u1 - l0].rearrange("p j (c i) -> p c j i", i=4)
+                dst = grouped[:, u0 - t0 : u1 - t0, j0:j1].rearrange("p (c i) j -> p c j i", i=4)
+                src = raw[i, l0, j0][:, :, u0 - l0 : u1 - l0].rearrange("p j (c i) -> p c j i", i=4)
                 if any(first <= u0 < end for first, end in SHARES[i]):
                     nc.vector.tensor_copy(out=dst, in_=src)
                 else:
                     nc.scalar.activation(dst, src, COPY)
-            return grouped
 
         def quantise(i, t0, t1, grouped):
             first_row = STEPS[i][1]
@@ -188,12 +191,18 @@ def tile_moe_ecr_lin_relu_kernel(
             )
 
         for i in range(len(STEPS)):
-            chunks = [(t0, t1, round_chunk(i, t0, t1)) for t0, t1 in QUANTS[i]]
+            chunks = [
+                (t0, t1, keep.tile([P, t1 - t0, PACK], BF16, name="grouped%d_%d" % (i, t0), align_bytes=64))
+                for t0, t1 in QUANTS[i]
+            ]
+            for j0, j1 in ROW_CUTS[i]:
+                for t0, t1, grouped in chunks:
+                    round_chunk(i, t0, t1, j0, j1, grouped)
             for t0, t1, grouped in chunks:
                 quantise(i, t0, t1, grouped)
             if i == 0:
                 gather_words(i, 0, S)
-            tag = "slot_lone" if i == 0 else "raw%d_%d" % (i, LOADS[i][-1][0])
+            tag = "slot_lone" if i == 0 else "raw%d_%d_0" % (i, LOADS[i][-1][0])
             part = LONE_PARTS[i]
             slot_lone.append(keep.tile([P, len(part) * C], U8, name="slot_lone%d" % i, tag=tag, align_bytes=64))
             nc.vector.tensor_copy(

@@ -39,10 +39,14 @@ LAST = len(STEPS) - 1
 HALF = T // 2
 THIRDS = [(t, t + CHUNK) for t in range(0, T, CHUNK)]
 HALVES = [(0, HALF), (HALF, T)]
-LOADS = [[(0, T)], [(0, T)], HALVES, THIRDS]
-ROW_CUTS = [((0, 2), (2, PACK))] + [((0, PACK),)] * LAST
+LOADS = [
+    [(0, 2, 0, T), (2, PACK, 0, 2 * CHUNK), (2, PACK, 2 * CHUNK, T)],
+    [(0, PACK, 0, T)],
+    [(0, PACK) + half for half in HALVES],
+    [(0, PACK) + third for third in THIRDS],
+]
 QUANTS = [THIRDS, THIRDS, THIRDS, THIRDS[:2] + [(512, 640), (640, 768)]]
-SHARES = [[(0, 448)], [(512, 768)], [(736, 768)], [(512, 640)]]
+SHARES = [[(0, 512), (0, 256), (512, 640)], [(448, 768)], [None, (704, 768)], [None, None, (512, 640)]]
 LONE_PARTS = ((0, 1, 2), (3,), (4,), (5,))
 GROUPS = ((0, 1, 2), (3, 4), (5,))
 BLOCKS = T // P
@@ -77,18 +81,13 @@ def tile_moe_ecr_lin_relu_kernel(
         ident = keep.tile([P, P], F32, name="ident")
         banks = [psum.tile([P, C], F32, name="bank%d" % e, tag="bank%d" % e) for e in range(E)]
         raw = {
-            (i, t0, j0): keep.tile(
-                [P, j1 - j0, t1 - t0],
-                F32,
-                name="raw%d_%d_%d" % (i, t0, j0),
-                tag="raw%d_%d_%d" % (i, t0, j0),
-                align_bytes=64,
+            (i, u): keep.tile(
+                [P, j1 - j0, t1 - t0], F32, name="raw%d_%d" % (i, u), tag="raw%d_%d" % (i, u), align_bytes=64
             )
             for i in range(len(STEPS))
-            for t0, t1 in LOADS[i]
-            for j0, j1 in ROW_CUTS[i]
+            for u, (j0, j1, t0, t1) in enumerate(LOADS[i])
         }
-        gate_loads = ((1, 0, HALF), (1, HALF, T), (2, 0, T))
+        gate_loads = ((1, 0, T), (2, 0, T))
         gates = [keep.tile([P, t1 - t0], F32, name="gate%d_%d" % (r, t0)) for r, t0, t1 in gate_loads]
         gate_rows = keep.tile([P, P], F32, name="gate_rows")
         turned_gate = keep.tile([P, BLOCKS], F32, name="turned_gate")
@@ -116,10 +115,9 @@ def tile_moe_ecr_lin_relu_kernel(
             load_bytes(w8[g][:], w8_words[group[0] : group[-1] + 1].rearrange("e a p n r -> p (e a) (n r)"))
 
         for i, (a, first_row) in enumerate(STEPS):
-            for t0, t1 in LOADS[i]:
-                rows = xT[a * K_PASS : (a + 1) * K_PASS, t0:t1].rearrange("(p j) w -> p j w", j=PACK)
-                for j0, j1 in ROW_CUTS[i]:
-                    nc.sync.dma_start(out=raw[i, t0, j0][:], in_=rows[:, j0:j1, :])
+            rows = xT[a * K_PASS : (a + 1) * K_PASS, :].rearrange("(p j) w -> p j w", j=PACK)
+            for u, (j0, j1, t0, t1) in enumerate(LOADS[i]):
+                nc.sync.dma_start(out=raw[i, u][:], in_=rows[:, j0:j1, t0:t1])
             if i == 0:
                 nc.sync.dma_start(offs_t[:], offs)
         nc.sync.dma_start(gate_rows[:BLOCKS, :], gate[0, 0, :].rearrange("(u t) -> u t", t=P))
@@ -141,13 +139,15 @@ def tile_moe_ecr_lin_relu_kernel(
         gate_bank = psum.tile([P, P], F32, name="gate_bank", tag="spare1")
         nc.tensor.transpose(gate_bank[:], gate_rows[:], ident[:])
 
-        def round_chunk(i, t0, t1, j0, j1, grouped):
-            cuts = sorted({t0, t1} | {t for pair in SHARES[i] + LOADS[i] for t in pair if t0 < t < t1})
+        def round_load(i, u, chunks):
+            j0, j1, l0, l1 = LOADS[i][u]
+            share = SHARES[i][u] or (l0, l0)
+            cuts = sorted({l0, l1, *share} | {t0 for t0, t1, grouped in chunks if l0 < t0 < l1})
             for u0, u1 in zip(cuts, cuts[1:]):
-                l0 = max(first for first, end in LOADS[i] if first <= u0)
+                t0, t1, grouped = [chunk for chunk in chunks if chunk[0] <= u0 < chunk[1]][0]
                 dst = grouped[:, u0 - t0 : u1 - t0, j0:j1].rearrange("p (c i) j -> p c j i", i=4)
-                src = raw[i, l0, j0][:, :, u0 - l0 : u1 - l0].rearrange("p j (c i) -> p c j i", i=4)
-                if any(first <= u0 < end for first, end in SHARES[i]):
+                src = raw[i, u][:, :, u0 - l0 : u1 - l0].rearrange("p j (c i) -> p c j i", i=4)
+                if share[0] <= u0 < share[1]:
                     nc.vector.tensor_copy(out=dst, in_=src)
                 else:
                     nc.scalar.activation(dst, src, COPY)
@@ -195,14 +195,13 @@ def tile_moe_ecr_lin_relu_kernel(
                 (t0, t1, keep.tile([P, t1 - t0, PACK], BF16, name="grouped%d_%d" % (i, t0), align_bytes=64))
                 for t0, t1 in QUANTS[i]
             ]
-            for j0, j1 in ROW_CUTS[i]:
-                for t0, t1, grouped in chunks:
-                    round_chunk(i, t0, t1, j0, j1, grouped)
+            for u in range(len(LOADS[i])):
+                round_load(i, u, chunks)
             for t0, t1, grouped in chunks:
                 quantise(i, t0, t1, grouped)
             if i == 0:
                 gather_words(i, 0, S)
-            tag = "slot_lone" if i == 0 else "raw%d_%d_0" % (i, LOADS[i][-1][0])
+            tag = "slot_lone" if i == 0 else "raw%d_%d" % (i, len(LOADS[i]) - 1)
             part = LONE_PARTS[i]
             slot_lone.append(keep.tile([P, len(part) * C], U8, name="slot_lone%d" % i, tag=tag, align_bytes=64))
             nc.vector.tensor_copy(
@@ -260,14 +259,13 @@ def tile_moe_ecr_lin_relu_kernel(
                 nc.scalar.activation(scaled[:, block], source, COPY, scale=turned_gate[:, t // P : t // P + 1])
                 nc.tensor.transpose(backs[h][:, block], scaled[:, block], ident[:])
 
-        parts = {}
-        for r in (1, 2):
-            for t0, t1 in HALVES:
-                parts[r, t0] = keep.tile([P, HALF], F32, name="part%d_%d" % (r, t0))
-                product(r, t0, t1, parts[r, t0][:])
+        second = keep.tile([P, T], F32, name="second")
         pair = keep.tile([P, T], F32, name="pair")
+        product(1, 0, T, second[:])
         for t0, t1 in HALVES:
-            nc.vector.tensor_tensor(pair[:, t0:t1], parts[1, t0][:], parts[2, t0][:], ADD)
+            product(2, t0, t1, pair[:, t0:t1])
+        for t0, t1 in HALVES:
+            nc.vector.tensor_tensor(pair[:, t0:t1], pair[:, t0:t1], second[:, t0:t1], ADD)
         for h, (t0, t1) in enumerate(HALVES):
             total = keep.tile([P, t1 - t0], F32, name="total%d" % h)
             nc.vector.tensor_tensor(total[:], pair[:, t0:t1], backs[h][:], ADD)

@@ -40,15 +40,21 @@ HALF = T // 2
 THIRDS = [(t, t + CHUNK) for t in range(0, T, CHUNK)]
 HALVES = [(0, HALF), (HALF, T)]
 LOADS = [
-    [(0, 2, 0, T), (2, PACK, 0, 2 * CHUNK), (2, PACK, 2 * CHUNK, T)],
+    [(0, PACK, 0, 2 * CHUNK), (0, PACK, 2 * CHUNK, T)],
     [(0, PACK, 0, T)],
     [(0, PACK) + half for half in HALVES],
     [(0, PACK) + third for third in THIRDS],
 ]
-QUANTS = [THIRDS, THIRDS, THIRDS, THIRDS[:2] + [(512, 640), (640, 768)]]
-SHARES = [[(0, 512), (0, 256), (512, 640)], [(448, 768)], [None, (704, 768)], [None, None, (512, 640)]]
+QUANTS = [
+    THIRDS[:2] + [(512, 640), (640, 768)],
+    [(384, 640), (640, 768), (0, 256), (256, 384)],
+    THIRDS,
+    THIRDS[:2] + [(t, t + 64) for t in range(2 * CHUNK, T, 64)],
+]
+SHARES = [[(0, 320), (512, 640)], [(384, 768)], [None, (704, 768)], [None, None, (512, 640)]]
 LONE_PARTS = ((0, 1, 2), (3,), (4,), (5,))
 GROUPS = ((0, 1, 2), (3, 4), (5,))
+SPANS = ((0, 384), (384, 640), (640, T))
 BLOCKS = T // P
 
 
@@ -250,7 +256,7 @@ def tile_moe_ecr_lin_relu_kernel(
             for u in range(0, CHUNK, P):
                 nc.tensor.transpose(turned[h][:, u : u + P], fetched[:, u : u + P], ident[:])
         backs = []
-        for h, (t0, t1) in enumerate(HALVES):
+        for h, (t0, t1) in enumerate(SPANS):
             scaled = keep.tile([P, t1 - t0], F32, name="scaled%d" % h)
             backs.append(psum.tile([P, t1 - t0], F32, name="back%d" % h, tag="bank%d" % (CHUNKS + h)))
             for t in range(t0, t1, P):
@@ -262,11 +268,15 @@ def tile_moe_ecr_lin_relu_kernel(
         second = keep.tile([P, T], F32, name="second")
         pair = keep.tile([P, T], F32, name="pair")
         product(1, 0, T, second[:])
-        for t0, t1 in HALVES:
-            product(2, t0, t1, pair[:, t0:t1])
-        for t0, t1 in HALVES:
-            nc.vector.tensor_tensor(pair[:, t0:t1], pair[:, t0:t1], second[:, t0:t1], ADD)
-        for h, (t0, t1) in enumerate(HALVES):
-            total = keep.tile([P, t1 - t0], F32, name="total%d" % h)
-            nc.vector.tensor_tensor(total[:], pair[:, t0:t1], backs[h][:], ADD)
-            nc.sync.dma_start(out=out[:, t0:t1], in_=total[:])
+        for stage in range(len(SPANS) + 3):
+            if stage < len(SPANS):
+                t0, t1 = SPANS[stage]
+                product(2, t0, t1, pair[:, t0:t1])
+            if 0 <= stage - 3 < len(SPANS):
+                t0, t1 = SPANS[stage - 3]
+                total = keep.tile([P, t1 - t0], F32, name="total%d" % t0)
+                nc.vector.tensor_tensor(total[:], pair[:, t0:t1], backs[stage - 3][:], ADD)
+                nc.sync.dma_start(out=out[:, t0:t1], in_=total[:])
+            if 0 <= stage - 1 < len(SPANS):
+                t0, t1 = SPANS[stage - 1]
+                nc.vector.tensor_tensor(pair[:, t0:t1], pair[:, t0:t1], second[:, t0:t1], ADD)

@@ -49,9 +49,9 @@ QUANTS = [
     THIRDS[:2] + [(512, 640), (640, 768)],
     [(384, 640), (640, 768), (0, 256), (256, 384)],
     THIRDS,
-    THIRDS[:2] + [(t, t + 64) for t in range(2 * CHUNK, T, 64)],
+    THIRDS[:2] + [(576, 704), (512, 576), (704, 768)],
 ]
-SHARES = [[(0, 320), (512, 640)], [(384, 768)], [None, (704, 768)], [None, None, (512, 640)]]
+SHARES = [[(0, 320), (512, 640)], [(384, 768)], [None, (704, 768)], [None, None, (512, 576)]]
 LONE_PARTS = ((0, 1, 2), (3,), (4,), (5,))
 GROUPS = ((0, 1, 2), (3, 4), (5,))
 SPANS = ((0, 384), (384, 640), (640, T))

@@ -36,24 +36,18 @@ WINDOW = 1024
 
 STEPS = ((2, 0), (0, 4), (1, 8), (3, 0))
 LAST = len(STEPS) - 1
-HALF = T // 2
 THIRDS = [(t, t + CHUNK) for t in range(0, T, CHUNK)]
-HALVES = [(0, HALF), (HALF, T)]
-LOADS = [
-    [(0, PACK, 0, 2 * CHUNK), (0, PACK, 2 * CHUNK, T)],
-    [(0, PACK, 0, T)],
-    [(0, PACK) + half for half in HALVES],
-    [(0, PACK) + third for third in THIRDS],
-]
-QUANTS = [
-    THIRDS[:2] + [(512, 640), (640, 768)],
-    [(384, 640), (640, 768), (0, 256), (256, 384)],
-    THIRDS,
-    THIRDS[:2] + [(576, 704), (512, 576), (704, 768)],
-]
-SHARES = [[(0, 320), (512, 640)], [(384, 768)], [None, (704, 768)], [None, None, (512, 576)]]
+RUN_CUTS = ((0, 512, T), (0, 256, T), (0, 256, T))
+SHARES = (((0, 256), (512, 640)), ((576, 768),), ((576, 768),), ((512, 576),))
+QUANTS = (
+    ((0, 256), (256, 512), (512, 640), (640, 768)),
+    ((0, 256), (512, 768), (256, 512)),
+    ((0, 256), (512, 768), (256, 512)),
+    ((0, 256), (256, 512), (576, 704), (512, 576), (704, 768)),
+)
 LONE_PARTS = ((0, 1, 2), (3,), (4,), (5,))
 GROUPS = ((0, 1, 2), (3, 4), (5,))
+W8_LOADS = ((0, 1, 2), (3, 4, 5))
 SPANS = ((0, 384), (384, 640), (640, T))
 BLOCKS = T // P
 
@@ -78,7 +72,7 @@ def tile_moe_ecr_lin_relu_kernel(
         slot_words = [keep.tile([P, S], U32, name="slot_words%d" % i, align_bytes=64) for i in range(len(STEPS))]
         slot_shared = keep.tile([P, S], U8, name="slot_shared", align_bytes=64)
         slot_lone = []
-        w8 = [keep.tile([P, FP8_PASSES * len(g), 4 * N], U8, name="w8_%d" % g[0], align_bytes=64) for g in GROUPS]
+        w8 = [keep.tile([P, FP8_PASSES * len(g), 4 * N], U8, name="w8_%d" % g[0], align_bytes=64) for g in W8_LOADS]
         w4 = [keep.tile([P, E, 2 * N], U8, name="w4_%d" % a, align_bytes=64) for a in range(2)]
         w8_planes = keep.tile([P, 2 * E, N], U8, name="w8_planes", align_bytes=64)
         w4_planes = keep.tile([P, 2 * E, N], U8, name="w4_planes", align_bytes=64)
@@ -86,13 +80,11 @@ def tile_moe_ecr_lin_relu_kernel(
         y = keep.tile([P, S + PAD], F32, name="y")
         ident = keep.tile([P, P], F32, name="ident")
         banks = [psum.tile([P, C], F32, name="bank%d" % e, tag="bank%d" % e) for e in range(E)]
-        raw = {
-            (i, u): keep.tile(
-                [P, j1 - j0, t1 - t0], F32, name="raw%d_%d" % (i, u), tag="raw%d_%d" % (i, u), align_bytes=64
-            )
-            for i in range(len(STEPS))
-            for u, (j0, j1, t0, t1) in enumerate(LOADS[i])
-        }
+        raw = [keep.tile([P, PACK * T], F32, name="raw%d" % i, tag="raw%d" % i, align_bytes=64) for i in range(LAST)]
+        raw_thirds = [
+            keep.tile([P, PACK, CHUNK], F32, name="third%d" % u, tag="third%d" % u, align_bytes=64)
+            for u in range(CHUNKS)
+        ]
         gate_loads = ((1, 0, T), (2, 0, T))
         gates = [keep.tile([P, t1 - t0], F32, name="gate%d_%d" % (r, t0)) for r, t0, t1 in gate_loads]
         gate_rows = keep.tile([P, P], F32, name="gate_rows")
@@ -117,13 +109,19 @@ def tile_moe_ecr_lin_relu_kernel(
                 load_bytes(dst[r:P:QUADRANT, :, :], rows[r])
 
         def load_w8(g):
-            group = GROUPS[g]
+            group = W8_LOADS[g]
             load_bytes(w8[g][:], w8_words[group[0] : group[-1] + 1].rearrange("e a p n r -> p (e a) (n r)"))
 
         for i, (a, first_row) in enumerate(STEPS):
             rows = xT[a * K_PASS : (a + 1) * K_PASS, :].rearrange("(p j) w -> p j w", j=PACK)
-            for u, (j0, j1, t0, t1) in enumerate(LOADS[i]):
-                nc.sync.dma_start(out=raw[i, u][:], in_=rows[:, j0:j1, t0:t1])
+            if i < LAST:
+                run = rows.rearrange("p j w -> p (j w)")
+                ends = [0] + [(PACK - 1) * T + t for t in RUN_CUTS[i][1:]]
+                for m0, m1 in zip(ends, ends[1:]):
+                    nc.sync.dma_start(out=raw[i][:, m0:m1], in_=run[:, m0:m1])
+            else:
+                for u, (t0, t1) in enumerate(THIRDS):
+                    nc.sync.dma_start(out=raw_thirds[u][:], in_=rows[:, :, t0:t1])
             if i == 0:
                 nc.sync.dma_start(offs_t[:], offs)
         nc.sync.dma_start(gate_rows[:BLOCKS, :], gate[0, 0, :].rearrange("(u t) -> u t", t=P))
@@ -135,7 +133,6 @@ def tile_moe_ecr_lin_relu_kernel(
         nc.sync.dma_start(bias[:], b)
         load_w8(1)
         load_bytes(w4[1][:], w4_by_pass[1])
-        load_w8(2)
         nc.sync.dma_start(pos_t[0][:], pos1)
         nc.sync.dma_start(pos_t[1][:], pos2)
         for tile, (r, t0, t1) in zip(gates, gate_loads):
@@ -145,15 +142,21 @@ def tile_moe_ecr_lin_relu_kernel(
         gate_bank = psum.tile([P, P], F32, name="gate_bank", tag="spare1")
         nc.tensor.transpose(gate_bank[:], gate_rows[:], ident[:])
 
-        def round_load(i, u, chunks):
-            j0, j1, l0, l1 = LOADS[i][u]
-            share = SHARES[i][u] or (l0, l0)
-            cuts = sorted({l0, l1, *share} | {t0 for t0, t1, grouped in chunks if l0 < t0 < l1})
-            for u0, u1 in zip(cuts, cuts[1:]):
-                t0, t1, grouped = [chunk for chunk in chunks if chunk[0] <= u0 < chunk[1]][0]
-                dst = grouped[:, u0 - t0 : u1 - t0, j0:j1].rearrange("p (c i) j -> p c j i", i=4)
-                src = raw[i, u][:, :, u0 - l0 : u1 - l0].rearrange("p j (c i) -> p c j i", i=4)
-                if share[0] <= u0 < share[1]:
+        def round_step(i, chunks):
+            edges = {t for share in SHARES[i] for t in share}
+            pieces = []
+            for t0, t1, grouped in chunks:
+                cuts = [t0] + sorted(t for t in edges if t0 < t < t1) + [t1]
+                pieces.extend((u0, u1, t0, grouped) for u0, u1 in zip(cuts, cuts[1:]))
+            for u0, u1, t0, grouped in pieces:
+                if i < LAST:
+                    src = raw[i][:].rearrange("p (j w) -> p j w", j=PACK)[:, :, u0:u1]
+                else:
+                    first = u0 // CHUNK * CHUNK
+                    src = raw_thirds[u0 // CHUNK][:, :, u0 - first : u1 - first]
+                dst = grouped[:, u0 - t0 : u1 - t0, :].rearrange("p (c i) j -> p c j i", i=4)
+                src = src.rearrange("p j (c i) -> p c j i", i=4)
+                if any(s0 <= u0 < s1 for s0, s1 in SHARES[i]):
                     nc.vector.tensor_copy(out=dst, in_=src)
                 else:
                     nc.scalar.activation(dst, src, COPY)
@@ -174,8 +177,8 @@ def tile_moe_ecr_lin_relu_kernel(
             a, first_row = STEPS[i]
             slots = slice(e * C, (e + 1) * C)
             if a < FP8_PASSES:
-                g = [e in group for group in GROUPS].index(True)
-                lhsT = w8[g][:, FP8_PASSES * (e - GROUPS[g][0]) + a, :].bitcast(FP8X4)
+                g = [e in group for group in W8_LOADS].index(True)
+                lhsT = w8[g][:, FP8_PASSES * (e - W8_LOADS[g][0]) + a, :].bitcast(FP8X4)
                 lhsT_scale = w8_planes[:, 2 * e + a, :]
             else:
                 lhsT = w4[a - FP8_PASSES][:, e, :].bitcast(FP4X4)
@@ -201,13 +204,12 @@ def tile_moe_ecr_lin_relu_kernel(
                 (t0, t1, keep.tile([P, t1 - t0, PACK], BF16, name="grouped%d_%d" % (i, t0), align_bytes=64))
                 for t0, t1 in QUANTS[i]
             ]
-            for u in range(len(LOADS[i])):
-                round_load(i, u, chunks)
+            round_step(i, chunks)
             for t0, t1, grouped in chunks:
                 quantise(i, t0, t1, grouped)
             if i == 0:
                 gather_words(i, 0, S)
-            tag = "slot_lone" if i == 0 else "raw%d_%d" % (i, len(LOADS[i]) - 1)
+            tag = ("slot_lone", "raw1", "raw2", "third%d" % (CHUNKS - 1))[i]
             part = LONE_PARTS[i]
             slot_lone.append(keep.tile([P, len(part) * C], U8, name="slot_lone%d" % i, tag=tag, align_bytes=64))
             nc.vector.tensor_copy(

@@ -36,13 +36,14 @@ WINDOW = 1024
 
 STEPS = ((2, 0), (0, 4), (1, 8), (3, 0))
 LAST = len(STEPS) - 1
+RUNS = 2
 THIRDS = [(t, t + CHUNK) for t in range(0, T, CHUNK)]
-RUN_CUTS = ((0, 512, T), (0, 256, T), (0, 256, T))
-SHARES = (((0, 256), (512, 640)), ((576, 768),), ((576, 768),), ((512, 576),))
+CUTS = ((0, 384, T), (0, 256, T), (0, 384, T), (0, 256, 512, T))
+SHARES = (((176, 384), (560, 768)), ((576, 768),), ((704, 768),), ((512, 576),))
 QUANTS = (
-    ((0, 256), (256, 512), (512, 640), (640, 768)),
+    ((0, 384), (512, 768), (384, 512)),
     ((0, 256), (512, 768), (256, 512)),
-    ((0, 256), (512, 768), (256, 512)),
+    ((0, 256), (256, 512), (512, 768)),
     ((0, 256), (256, 512), (576, 704), (512, 576), (704, 768)),
 )
 LONE_PARTS = ((0, 1, 2), (3,), (4,), (5,))
@@ -80,11 +81,12 @@ def tile_moe_ecr_lin_relu_kernel(
         y = keep.tile([P, S + PAD], F32, name="y")
         ident = keep.tile([P, P], F32, name="ident")
         banks = [psum.tile([P, C], F32, name="bank%d" % e, tag="bank%d" % e) for e in range(E)]
-        raw = [keep.tile([P, PACK * T], F32, name="raw%d" % i, tag="raw%d" % i, align_bytes=64) for i in range(LAST)]
-        raw_thirds = [
-            keep.tile([P, PACK, CHUNK], F32, name="third%d" % u, tag="third%d" % u, align_bytes=64)
-            for u in range(CHUNKS)
-        ]
+        spans = [[(0, T)] if i < RUNS else list(zip(cuts, cuts[1:])) for i, cuts in enumerate(CUTS)]
+        raw = {
+            (i, t0): keep.tile([P, PACK * (t1 - t0)], F32, name="raw%d_%d" % (i, t0), tag="raw%d_%d" % (i, t0), align_bytes=64)
+            for i in range(len(STEPS))
+            for t0, t1 in spans[i]
+        }
         gate_loads = ((1, 0, T), (2, 0, T))
         gates = [keep.tile([P, t1 - t0], F32, name="gate%d_%d" % (r, t0)) for r, t0, t1 in gate_loads]
         gate_rows = keep.tile([P, P], F32, name="gate_rows")
@@ -114,14 +116,14 @@ def tile_moe_ecr_lin_relu_kernel(
 
         for i, (a, first_row) in enumerate(STEPS):
             rows = xT[a * K_PASS : (a + 1) * K_PASS, :].rearrange("(p j) w -> p j w", j=PACK)
-            if i < LAST:
+            if i < RUNS:
                 run = rows.rearrange("p j w -> p (j w)")
-                ends = [0] + [(PACK - 1) * T + t for t in RUN_CUTS[i][1:]]
+                ends = [0] + [(PACK - 1) * T + t for t in CUTS[i][1:]]
                 for m0, m1 in zip(ends, ends[1:]):
-                    nc.sync.dma_start(out=raw[i][:, m0:m1], in_=run[:, m0:m1])
+                    nc.sync.dma_start(out=raw[i, 0][:, m0:m1], in_=run[:, m0:m1])
             else:
-                for u, (t0, t1) in enumerate(THIRDS):
-                    nc.sync.dma_start(out=raw_thirds[u][:], in_=rows[:, :, t0:t1])
+                for t0, t1 in spans[i]:
+                    nc.sync.dma_start(out=raw[i, t0][:].rearrange("p (j w) -> p j w", j=PACK), in_=rows[:, :, t0:t1])
             if i == 0:
                 nc.sync.dma_start(offs_t[:], offs)
         nc.sync.dma_start(gate_rows[:BLOCKS, :], gate[0, 0, :].rearrange("(u t) -> u t", t=P))
@@ -143,17 +145,14 @@ def tile_moe_ecr_lin_relu_kernel(
         nc.tensor.transpose(gate_bank[:], gate_rows[:], ident[:])
 
         def round_step(i, chunks):
-            edges = {t for share in SHARES[i] for t in share}
+            edges = {t for share in SHARES[i] for t in share} | set(CUTS[i])
             pieces = []
             for t0, t1, grouped in chunks:
                 cuts = [t0] + sorted(t for t in edges if t0 < t < t1) + [t1]
                 pieces.extend((u0, u1, t0, grouped) for u0, u1 in zip(cuts, cuts[1:]))
             for u0, u1, t0, grouped in pieces:
-                if i < LAST:
-                    src = raw[i][:].rearrange("p (j w) -> p j w", j=PACK)[:, :, u0:u1]
-                else:
-                    first = u0 // CHUNK * CHUNK
-                    src = raw_thirds[u0 // CHUNK][:, :, u0 - first : u1 - first]
+                first = max(s0 for s0, s1 in spans[i] if s0 <= u0)
+                src = raw[i, first][:].rearrange("p (j w) -> p j w", j=PACK)[:, :, u0 - first : u1 - first]
                 dst = grouped[:, u0 - t0 : u1 - t0, :].rearrange("p (c i) j -> p c j i", i=4)
                 src = src.rearrange("p j (c i) -> p c j i", i=4)
                 if any(s0 <= u0 < s1 for s0, s1 in SHARES[i]):
@@ -209,7 +208,7 @@ def tile_moe_ecr_lin_relu_kernel(
                 quantise(i, t0, t1, grouped)
             if i == 0:
                 gather_words(i, 0, S)
-            tag = ("slot_lone", "raw1", "raw2", "third%d" % (CHUNKS - 1))[i]
+            tag = "slot_lone" if i == 0 else "raw%d_%d" % (i, spans[i][-1][0])
             part = LONE_PARTS[i]
             slot_lone.append(keep.tile([P, len(part) * C], U8, name="slot_lone%d" % i, tag=tag, align_bytes=64))
             nc.vector.tensor_copy(

@@ -39,12 +39,12 @@ LAST = len(STEPS) - 1
 RUNS = 2
 THIRDS = [(t, t + CHUNK) for t in range(0, T, CHUNK)]
 CUTS = ((0, 384, T), (0, 256, T), (0, 384, T), (0, 256, 512, T))
-SHARES = (((176, 384), (560, 768)), ((576, 768),), ((704, 768),), ((512, 576),))
+SHARES = (((144, 384), (576, 768)), ((512, 768),), ((704, 768),), ((512, 640),))
 QUANTS = (
     ((0, 384), (512, 768), (384, 512)),
     ((0, 256), (512, 768), (256, 512)),
     ((0, 256), (256, 512), (512, 768)),
-    ((0, 256), (256, 512), (576, 704), (512, 576), (704, 768)),
+    ((0, 256), (256, 512), (512, 640), (640, 768)),
 )
 LONE_PARTS = ((0, 1, 2), (3,), (4,), (5,))
 GROUPS = ((0, 1, 2), (3, 4), (5,))

@@ -34,7 +34,7 @@ CHUNK = 256
 CHUNKS = T // CHUNK
 WINDOW = 1024
 
-STEPS = ((2, 0), (0, 4), (1, 8), (3, 0))
+STEPS = ((2, 0), (3, 0), (0, 4), (1, 8))
 LAST = len(STEPS) - 1
 RUNS = 2
 THIRDS = [(t, t + CHUNK) for t in range(0, T, CHUNK)]
@@ -48,7 +48,7 @@ QUANTS = (
 )
 LONE_PARTS = ((0, 1, 2), (3,), (4,), (5,))
 GROUPS = ((0, 1, 2), (3, 4), (5,))
-W8_LOADS = ((0, 1, 2), (3, 4, 5))
+W8_LOADS = ((0, 0, 6), (1, 0, 4), (1, 4, 6))
 SPANS = ((0, 384), (384, 640), (640, T))
 BLOCKS = T // P
 
@@ -73,8 +73,8 @@ def tile_moe_ecr_lin_relu_kernel(
         slot_words = [keep.tile([P, S], U32, name="slot_words%d" % i, align_bytes=64) for i in range(len(STEPS))]
         slot_shared = keep.tile([P, S], U8, name="slot_shared", align_bytes=64)
         slot_lone = []
-        w8 = [keep.tile([P, FP8_PASSES * len(g), 4 * N], U8, name="w8_%d" % g[0], align_bytes=64) for g in W8_LOADS]
-        w4 = [keep.tile([P, E, 2 * N], U8, name="w4_%d" % a, align_bytes=64) for a in range(2)]
+        w8 = [keep.tile([P, e1 - e0, 4 * N], U8, name="w8_%d_%d" % (a, e0), align_bytes=64) for a, e0, e1 in W8_LOADS]
+        w4 = keep.tile([P, 2 * E, 2 * N], U8, name="w4", align_bytes=64)
         w8_planes = keep.tile([P, 2 * E, N], U8, name="w8_planes", align_bytes=64)
         w4_planes = keep.tile([P, 2 * E, N], U8, name="w4_planes", align_bytes=64)
         bias = keep.tile([P, E], F32, name="bias")
@@ -110,10 +110,6 @@ def tile_moe_ecr_lin_relu_kernel(
             for r in range(ROWS):
                 load_bytes(dst[r:P:QUADRANT, :, :], rows[r])
 
-        def load_w8(g):
-            group = W8_LOADS[g]
-            load_bytes(w8[g][:], w8_words[group[0] : group[-1] + 1].rearrange("e a p n r -> p (e a) (n r)"))
-
         for i, (a, first_row) in enumerate(STEPS):
             rows = xT[a * K_PASS : (a + 1) * K_PASS, :].rearrange("(p j) w -> p j w", j=PACK)
             if i < RUNS:
@@ -127,14 +123,13 @@ def tile_moe_ecr_lin_relu_kernel(
             if i == 0:
                 nc.sync.dma_start(offs_t[:], offs)
         nc.sync.dma_start(gate_rows[:BLOCKS, :], gate[0, 0, :].rearrange("(u t) -> u t", t=P))
-        w4_by_pass = w4_words.rearrange("e a p m -> a p e m")
         load_planes(w4_planes, w4_scales)
-        load_bytes(w4[0][:], w4_by_pass[0])
-        load_w8(0)
+        load_bytes(w4[:], w4_words.rearrange("e a p m -> p (e a) m"))
         load_planes(w8_planes, w8_scales)
         nc.sync.dma_start(bias[:], b)
-        load_w8(1)
-        load_bytes(w4[1][:], w4_by_pass[1])
+        w8_by_pass = w8_words.rearrange("e a p n r -> a p e (n r)")
+        for tile, (a, e0, e1) in zip(w8, W8_LOADS):
+            load_bytes(tile[:], w8_by_pass[a][:, e0:e1, :])
         nc.sync.dma_start(pos_t[0][:], pos1)
         nc.sync.dma_start(pos_t[1][:], pos2)
         for tile, (r, t0, t1) in zip(gates, gate_loads):
@@ -176,11 +171,11 @@ def tile_moe_ecr_lin_relu_kernel(
             a, first_row = STEPS[i]
             slots = slice(e * C, (e + 1) * C)
             if a < FP8_PASSES:
-                g = [e in group for group in W8_LOADS].index(True)
-                lhsT = w8[g][:, FP8_PASSES * (e - W8_LOADS[g][0]) + a, :].bitcast(FP8X4)
+                g = [a == q and e0 <= e < e1 for q, e0, e1 in W8_LOADS].index(True)
+                lhsT = w8[g][:, e - W8_LOADS[g][1], :].bitcast(FP8X4)
                 lhsT_scale = w8_planes[:, 2 * e + a, :]
             else:
-                lhsT = w4[a - FP8_PASSES][:, e, :].bitcast(FP4X4)
+                lhsT = w4[:, 2 * e + a - FP8_PASSES, :].bitcast(FP4X4)
                 lhsT_scale = w4_planes[:, 2 * e + a - FP8_PASSES, :]
             if i == 0:
                 g = [e in part for part in LONE_PARTS].index(True)
@@ -219,22 +214,13 @@ def tile_moe_ecr_lin_relu_kernel(
         nc.scalar.copy(turned_gate[:], gate_bank[:, :BLOCKS])
         for e in range(E):
             multiply(0, e)
-        idle = psum.tile([P, 2 * N], F32, name="idle", tag="spare0")
-        nc.tensor.matmul_mx(
-            out=idle[:],
-            lhsT=w8[0][:, 0, :].bitcast(FP8X4),
-            lhsT_scale=w4_planes[:, 0, :],
-            rhs=w8[0][:, :2, :].rearrange("p a m -> p (a m)").bitcast(FP8X4),
-            rhs_scale=w4_planes[:, :2, :].rearrange("p a n -> p (a n)"),
-            start=True,
-            stop=True,
-        )
         for h in range(2):
             s0, s1 = h * S // 2, (h + 1) * S // 2
             nc.vector.tensor_copy(slot_shared[:, s0:s1], shared_planes[:].indirect(entries(offs_t, s0, s1)))
             for e in range(s0 // C, s1 // C):
-                for i in range(1, LAST):
-                    multiply(i, e)
+                multiply(1, e)
+        for e in range(E):
+            multiply(2, e)
         for group in GROUPS:
             gather_words(LAST, group[0] * C, (group[-1] + 1) * C)
             for e in group:

@@ -148,9 +148,11 @@ def tile_moe_ecr_lin_relu_kernel(
             for u0, u1, t0, grouped in pieces:
                 first = max(s0 for s0, s1 in spans[i] if s0 <= u0)
                 src = raw[i, first][:].rearrange("p (j w) -> p j w", j=PACK)[:, :, u0 - first : u1 - first]
-                dst = grouped[:, u0 - t0 : u1 - t0, :].rearrange("p (c i) j -> p c j i", i=4)
-                src = src.rearrange("p j (c i) -> p c j i", i=4)
-                if any(s0 <= u0 < s1 for s0, s1 in SHARES[i]):
+                on_vector = any(s0 <= u0 < s1 for s0, s1 in SHARES[i])
+                run = 4 if on_vector else 2
+                dst = grouped[:, u0 - t0 : u1 - t0, :].rearrange("p (c i) j -> p c j i", i=run)
+                src = src.rearrange("p j (c i) -> p c j i", i=run)
+                if on_vector:
                     nc.vector.tensor_copy(out=dst, in_=src)
                 else:
                     nc.scalar.activation(dst, src, COPY)

@@ -232,6 +232,17 @@ def tile_moe_ecr_lin_relu_kernel(
                 else:
                     nc.vector.tensor_scalar(y[:, e * C : (e + 1) * C], banks[e][:], bias[:, e : e + 1], 0.0, ADD, MAX)
 
+        idle = psum.tile([P, 2 * C], F32, name="idle", tag="spare0")
+        nc.tensor.matmul_mx(
+            out=idle[:],
+            lhsT=w8[-1][:, 0, :].bitcast(FP8X4),
+            lhsT_scale=w8_planes[:, 0, :],
+            rhs=slot_words[LAST][:, S - 2 * C :].bitcast(FP8X4),
+            rhs_scale=slot_shared[STEPS[LAST][1] : P, S - 2 * C :],
+            start=True,
+            stop=True,
+        )
+
         def product(r, t0, t1, part):
             j = [r == q and u0 <= t0 < u1 for q, u0, u1 in gate_loads].index(True)
             weights = gates[j][:, t0 - gate_loads[j][1] : t1 - gate_loads[j][1]]

@@ -48,7 +48,7 @@ QUANTS = (
 )
 LONE_PARTS = ((0, 1, 2), (3,), (4,), (5,))
 GROUPS = ((0, 1, 2), (3, 4), (5,))
-W8_LOADS = ((0, 0, 6), (1, 0, 4), (1, 4, 6))
+W8_LOADS = ((0, 0, 3), (0, 3, 6), (1, 0, 3), (1, 3, 5), (1, 5, 6))
 SPANS = ((0, 384), (384, 640), (640, T))
 BLOCKS = T // P
 
@@ -74,7 +74,7 @@ def tile_moe_ecr_lin_relu_kernel(
         slot_shared = keep.tile([P, S], U8, name="slot_shared", align_bytes=64)
         slot_lone = []
         w8 = [keep.tile([P, e1 - e0, 4 * N], U8, name="w8_%d_%d" % (a, e0), align_bytes=64) for a, e0, e1 in W8_LOADS]
-        w4 = keep.tile([P, 2 * E, 2 * N], U8, name="w4", align_bytes=64)
+        w4 = [keep.tile([P, E, 2 * N], U8, name="w4_%d" % a, align_bytes=64) for a in range(2)]
         w8_planes = keep.tile([P, 2 * E, N], U8, name="w8_planes", align_bytes=64)
         w4_planes = keep.tile([P, 2 * E, N], U8, name="w4_planes", align_bytes=64)
         bias = keep.tile([P, E], F32, name="bias")
@@ -87,7 +87,7 @@ def tile_moe_ecr_lin_relu_kernel(
             for i in range(len(STEPS))
             for t0, t1 in spans[i]
         }
-        gate_loads = ((1, 0, T), (2, 0, T))
+        gate_loads = ((1, 0, CHUNK), (1, CHUNK, T)) + tuple((2, t0, t1) for t0, t1 in SPANS)
         gates = [keep.tile([P, t1 - t0], F32, name="gate%d_%d" % (r, t0)) for r, t0, t1 in gate_loads]
         gate_rows = keep.tile([P, P], F32, name="gate_rows")
         turned_gate = keep.tile([P, BLOCKS], F32, name="turned_gate")
@@ -123,8 +123,10 @@ def tile_moe_ecr_lin_relu_kernel(
             if i == 0:
                 nc.sync.dma_start(offs_t[:], offs)
         nc.sync.dma_start(gate_rows[:BLOCKS, :], gate[0, 0, :].rearrange("(u t) -> u t", t=P))
+        w4_by_pass = [w4_words.rearrange("e a p m -> a p e m")[a] for a in range(2)]
         load_planes(w4_planes, w4_scales)
-        load_bytes(w4[:], w4_words.rearrange("e a p m -> p (e a) m"))
+        for tile, words_of_pass in zip(w4, w4_by_pass):
+            load_bytes(tile[:], words_of_pass)
         load_planes(w8_planes, w8_scales)
         nc.sync.dma_start(bias[:], b)
         w8_by_pass = w8_words.rearrange("e a p n r -> a p e (n r)")
@@ -133,7 +135,7 @@ def tile_moe_ecr_lin_relu_kernel(
         nc.sync.dma_start(pos_t[0][:], pos1)
         nc.sync.dma_start(pos_t[1][:], pos2)
         for tile, (r, t0, t1) in zip(gates, gate_loads):
-            if r == 2:
+            if (r, t0) == (2, 0):
                 nc.sync.dma_start(pos_t[2][:], pos3)
             nc.sync.dma_start(tile[:], gate[r, :, t0:t1])
         gate_bank = psum.tile([P, P], F32, name="gate_bank", tag="spare1")
@@ -177,7 +179,7 @@ def tile_moe_ecr_lin_relu_kernel(
                 lhsT = w8[g][:, e - W8_LOADS[g][1], :].bitcast(FP8X4)
                 lhsT_scale = w8_planes[:, 2 * e + a, :]
             else:
-                lhsT = w4[:, 2 * e + a - FP8_PASSES, :].bitcast(FP4X4)
+                lhsT = w4[a - FP8_PASSES][:, e, :].bitcast(FP4X4)
                 lhsT_scale = w4_planes[:, 2 * e + a - FP8_PASSES, :]
             if i == 0:
                 g = [e in part for part in LONE_PARTS].index(True)
@@ -267,7 +269,8 @@ def tile_moe_ecr_lin_relu_kernel(
 
         second = keep.tile([P, T], F32, name="second")
         pair = keep.tile([P, T], F32, name="pair")
-        product(1, 0, T, second[:])
+        for r, t0, t1 in gate_loads[:2]:
+            product(r, t0, t1, second[:, t0:t1])
         for stage in range(len(SPANS) + 3):
             if stage < len(SPANS):
                 t0, t1 = SPANS[stage]

@@ -48,8 +48,10 @@ QUANTS = (
 )
 LONE_PARTS = ((0, 1, 2), (3,), (4,), (5,))
 GROUPS = ((0, 1, 2), (3, 4), (5,))
+W8_ROW = 8
 W8_LOADS = ((0, 0, 3), (0, 3, 6), (1, 0, 3), (1, 3, 5), (1, 5, 6))
 SPANS = ((0, 384), (384, 640), (640, T))
+STORES = ((0, 256), (256, 384), (384, 640), (640, T))
 BLOCKS = T // P
 
 
@@ -105,10 +107,10 @@ def tile_moe_ecr_lin_relu_kernel(
         def load_bytes(dst, src, queue=nc.sync):
             queue.dma_start(out=dst.bitcast(I32), in_=src.bitcast(I32))
 
-        def load_planes(dst, src):
+        def load_planes(dst, src, first_row):
             rows = src.rearrange("e a (q r) n -> r q (e a) n", r=ROWS)
             for r in range(ROWS):
-                load_bytes(dst[r:P:QUADRANT, :, :], rows[r])
+                load_bytes(dst[first_row + r : P : QUADRANT, :, :], rows[r])
 
         for i, (a, first_row) in enumerate(STEPS):
             rows = xT[a * K_PASS : (a + 1) * K_PASS, :].rearrange("(p j) w -> p j w", j=PACK)
@@ -124,10 +126,10 @@ def tile_moe_ecr_lin_relu_kernel(
                 nc.sync.dma_start(offs_t[:], offs)
         nc.sync.dma_start(gate_rows[:BLOCKS, :], gate[0, 0, :].rearrange("(u t) -> u t", t=P))
         w4_by_pass = [w4_words.rearrange("e a p m -> a p e m")[a] for a in range(2)]
-        load_planes(w4_planes, w4_scales)
+        load_planes(w4_planes, w4_scales, 0)
         for tile, words_of_pass in zip(w4, w4_by_pass):
             load_bytes(tile[:], words_of_pass)
-        load_planes(w8_planes, w8_scales)
+        load_planes(w8_planes, w8_scales, W8_ROW)
         nc.sync.dma_start(bias[:], b)
         w8_by_pass = w8_words.rearrange("e a p n r -> a p e (n r)")
         for tile, (a, e0, e1) in zip(w8, W8_LOADS):
@@ -177,7 +179,7 @@ def tile_moe_ecr_lin_relu_kernel(
             if a < FP8_PASSES:
                 g = [a == q and e0 <= e < e1 for q, e0, e1 in W8_LOADS].index(True)
                 lhsT = w8[g][:, e - W8_LOADS[g][1], :].bitcast(FP8X4)
-                lhsT_scale = w8_planes[:, 2 * e + a, :]
+                lhsT_scale = w8_planes[W8_ROW:P, 2 * e + a, :]
             else:
                 lhsT = w4[a - FP8_PASSES][:, e, :].bitcast(FP4X4)
                 lhsT_scale = w4_planes[:, 2 * e + a - FP8_PASSES, :]
@@ -238,7 +240,7 @@ def tile_moe_ecr_lin_relu_kernel(
         nc.tensor.matmul_mx(
             out=idle[:],
             lhsT=w8[-1][:, 0, :].bitcast(FP8X4),
-            lhsT_scale=w8_planes[:, 0, :],
+            lhsT_scale=w8_planes[W8_ROW:P, 0, :],
             rhs=slot_words[LAST][:, S - 2 * C :].bitcast(FP8X4),
             rhs_scale=slot_shared[STEPS[LAST][1] : P, S - 2 * C :],
             start=True,
@@ -258,9 +260,9 @@ def tile_moe_ecr_lin_relu_kernel(
             for u in range(0, CHUNK, P):
                 nc.tensor.transpose(turned[h][:, u : u + P], fetched[:, u : u + P], ident[:])
         backs = []
-        for h, (t0, t1) in enumerate(SPANS):
+        for h, (t0, t1) in enumerate(STORES):
             scaled = keep.tile([P, t1 - t0], F32, name="scaled%d" % h)
-            backs.append(psum.tile([P, t1 - t0], F32, name="back%d" % h, tag="bank%d" % (CHUNKS + h)))
+            backs.append(psum.tile([P, t1 - t0], F32, name="back%d" % h, tag="bank%d" % (CHUNKS + h) if h < CHUNKS else "spare1"))
             for t in range(t0, t1, P):
                 block = slice(t - t0, t - t0 + P)
                 source = turned[t // CHUNK][:, t % CHUNK : t % CHUNK + P]
@@ -271,15 +273,14 @@ def tile_moe_ecr_lin_relu_kernel(
         pair = keep.tile([P, T], F32, name="pair")
         for r, t0, t1 in gate_loads[:2]:
             product(r, t0, t1, second[:, t0:t1])
-        for stage in range(len(SPANS) + 3):
+        for stage in range(len(SPANS) + 2):
             if stage < len(SPANS):
                 t0, t1 = SPANS[stage]
                 product(2, t0, t1, pair[:, t0:t1])
-            if 0 <= stage - 3 < len(SPANS):
-                t0, t1 = SPANS[stage - 3]
-                total = keep.tile([P, t1 - t0], F32, name="total%d" % t0)
-                nc.vector.tensor_tensor(total[:], pair[:, t0:t1], backs[stage - 3][:], ADD)
-                nc.sync.dma_start(out=out[:, t0:t1], in_=total[:])
-            if 0 <= stage - 1 < len(SPANS):
-                t0, t1 = SPANS[stage - 1]
+            if 0 <= stage - 2 < len(SPANS):
+                t0, t1 = SPANS[stage - 2]
                 nc.vector.tensor_tensor(pair[:, t0:t1], pair[:, t0:t1], second[:, t0:t1], ADD)
+        for back, (t0, t1) in zip(backs, STORES):
+            total = keep.tile([P, t1 - t0], F32, name="total%d" % t0)
+            nc.vector.tensor_tensor(total[:], pair[:, t0:t1], back[:], ADD)
+            nc.sync.dma_start(out=out[:, t0:t1], in_=total[:])

from contextlib import ExitStack

import concourse.mybir as mybir
from concourse.masks import make_identity

K, T, E, C, N = 2048, 768, 6, 128, 128
TOP = 3
PAD = 64
S = E * C
FLOPS = 2 * K * N * S

F32 = mybir.dt.float32
BF16 = mybir.dt.bfloat16
I32 = mybir.dt.int32
U32 = mybir.dt.uint32
U16 = mybir.dt.uint16
U8 = mybir.dt.uint8
FP8X4 = mybir.dt.float8_e4m3fn_x4
FP4X4 = mybir.dt.float4_e2m1fn_x4
COPY = mybir.ActivationFunctionType.Copy
RELU = mybir.ActivationFunctionType.Relu
MULT = mybir.AluOpType.mult
ADD = mybir.AluOpType.add
MAX = mybir.AluOpType.max

P = 128
PACK = 4
K_PASS = P * PACK
FP8_PASSES = 2
QUADRANT = 32
ROWS = 4
LIST_ROWS = 16
CHUNK = 256
CHUNKS = T // CHUNK
WINDOW = 1024

STEPS = ((2, 0), (3, 0), (0, 4), (1, 8))
LAST = len(STEPS) - 1
RUNS = 2
THIRDS = [(t, t + CHUNK) for t in range(0, T, CHUNK)]
CUTS = ((0, 384, T), (0, 256, T), (0, 384, T), (0, 256, 512, T))
SHARES = (((144, 384), (576, 768)), ((512, 768),), ((704, 768),), ((512, 640),))
QUANTS = (
    ((0, 384), (512, 768), (384, 512)),
    ((0, 256), (512, 768), (256, 512)),
    ((0, 256), (256, 512), (512, 768)),
    ((0, 256), (256, 512), (512, 640), (640, 768)),
)
LONE_PARTS = ((0, 1, 2), (3,), (4,), (5,))
GROUPS = ((0, 1, 2), (3, 4), (5,))
W8_ROW = 8
W8_LOADS = ((0, 0, 3), (0, 3, 6), (1, 0, 3), (1, 3, 5), (1, 5, 6))
SPANS = ((0, 384), (384, 640), (640, T))
STORES = ((0, 256), (256, 384), (384, 640), (640, T))
BLOCKS = T // P


def entries(lst, first, end):
    return lst[:, first // LIST_ROWS : end // LIST_ROWS]


def tile_moe_ecr_lin_relu_kernel(
    tc, xT, w8_words, w8_scales, w4_words, w4_scales, b, gate, offs, pos1, pos2, pos3, out
):
    nc = tc.nc
    with ExitStack() as ctx:
        keep = ctx.enter_context(tc.tile_pool(name="keep", bufs=1))
        psum = ctx.enter_context(tc.psum_pool(name="psum", bufs=1))

        offs_t = keep.tile([P, S // LIST_ROWS], U16, name="offs_t")
        pos_t = [keep.tile([P, T // LIST_ROWS], U16, name="pos%d" % r) for r in range(TOP)]
        words = [keep.tile([P, WINDOW], I32, name="words%d" % i, align_bytes=64) for i in range(len(STEPS))]
        lone_plane = keep.tile([P, WINDOW], U8, name="lone_plane", align_bytes=64)
        shared_planes = keep.tile([P, WINDOW], U8, name="shared_planes", align_bytes=64)
        slot_words = [keep.tile([P, S], U32, name="slot_words%d" % i, align_bytes=64) for i in range(len(STEPS))]
        slot_shared = keep.tile([P, S], U8, name="slot_shared", align_bytes=64)
        slot_lone = []
        w8 = [keep.tile([P, e1 - e0, 4 * N], U8, name="w8_%d_%d" % (a, e0), align_bytes=64) for a, e0, e1 in W8_LOADS]
        w4 = [keep.tile([P, E, 2 * N], U8, name="w4_%d" % a, align_bytes=64) for a in range(2)]
        w8_planes = keep.tile([P, 2 * E, N], U8, name="w8_planes", align_bytes=64)
        w4_planes = keep.tile([P, 2 * E, N], U8, name="w4_planes", align_bytes=64)
        bias = keep.tile([P, E], F32, name="bias")
        y = keep.tile([P, S + PAD], F32, name="y")
        ident = keep.tile([P, P], F32, name="ident")
        banks = [psum.tile([P, C], F32, name="bank%d" % e, tag="bank%d" % e) for e in range(E)]
        spans = [[(0, T)] if i < RUNS else list(zip(cuts, cuts[1:])) for i, cuts in enumerate(CUTS)]
        raw = {
            (i, t0): keep.tile([P, PACK * (t1 - t0)], F32, name="raw%d_%d" % (i, t0), tag="raw%d_%d" % (i, t0), align_bytes=64)
            for i in range(len(STEPS))
            for t0, t1 in spans[i]
        }
        gate_loads = ((1, 0, CHUNK), (1, CHUNK, T)) + tuple((2, t0, t1) for t0, t1 in SPANS)
        gates = [keep.tile([P, t1 - t0], F32, name="gate%d_%d" % (r, t0)) for r, t0, t1 in gate_loads]
        gate_rows = keep.tile([P, P], F32, name="gate_rows")
        turned_gate = keep.tile([P, BLOCKS], F32, name="turned_gate")

        nc.vector.memset(w4_planes[:].rearrange("p a n -> p (a n)").bitcast(I32), 0)
        nc.vector.memset(w8_planes[:].rearrange("p a n -> p (a n)").bitcast(I32), 0)
        for plane in (lone_plane, shared_planes):
            nc.vector.memset(plane[:].bitcast(I32), 0)
        for step_words in words:
            nc.vector.memset(step_words[:, T:], 0)
        nc.vector.memset(y[:, S:], 0.0)
        nc.vector.memset(gate_rows[:], 0.0)
        make_identity(nc, ident[:])

        def load_bytes(dst, src, queue=nc.sync):
            queue.dma_start(out=dst.bitcast(I32), in_=src.bitcast(I32))

        def load_planes(dst, src, first_row):
            rows = src.rearrange("e a (q r) n -> r q (e a) n", r=ROWS)
            for r in range(ROWS):
                load_bytes(dst[first_row + r : P : QUADRANT, :, :], rows[r])

        for i, (a, first_row) in enumerate(STEPS):
            rows = xT[a * K_PASS : (a + 1) * K_PASS, :].rearrange("(p j) w -> p j w", j=PACK)
            if i < RUNS:
                run = rows.rearrange("p j w -> p (j w)")
                ends = [0] + [(PACK - 1) * T + t for t in CUTS[i][1:]]
                for m0, m1 in zip(ends, ends[1:]):
                    nc.sync.dma_start(out=raw[i, 0][:, m0:m1], in_=run[:, m0:m1])
            else:
                for t0, t1 in spans[i]:
                    nc.sync.dma_start(out=raw[i, t0][:].rearrange("p (j w) -> p j w", j=PACK), in_=rows[:, :, t0:t1])
            if i == 0:
                nc.sync.dma_start(offs_t[:], offs)
        nc.sync.dma_start(gate_rows[:BLOCKS, :], gate[0, 0, :].rearrange("(u t) -> u t", t=P))
        w4_by_pass = [w4_words.rearrange("e a p m -> a p e m")[a] for a in range(2)]
        load_planes(w4_planes, w4_scales, 0)
        for tile, words_of_pass in zip(w4, w4_by_pass):
            load_bytes(tile[:], words_of_pass)
        load_planes(w8_planes, w8_scales, W8_ROW)
        nc.sync.dma_start(bias[:], b)
        w8_by_pass = w8_words.rearrange("e a p n r -> a p e (n r)")
        for tile, (a, e0, e1) in zip(w8, W8_LOADS):
            load_bytes(tile[:], w8_by_pass[a][:, e0:e1, :])
        nc.sync.dma_start(pos_t[0][:], pos1)
        nc.sync.dma_start(pos_t[1][:], pos2)
        for tile, (r, t0, t1) in zip(gates, gate_loads):
            if (r, t0) == (2, 0):
                nc.sync.dma_start(pos_t[2][:], pos3)
            nc.sync.dma_start(tile[:], gate[r, :, t0:t1])
        gate_bank = psum.tile([P, P], F32, name="gate_bank", tag="spare1")
        nc.tensor.transpose(gate_bank[:], gate_rows[:], ident[:])

        def round_step(i, chunks):
            edges = {t for share in SHARES[i] for t in share} | set(CUTS[i])
            pieces = []
            for t0, t1, grouped in chunks:
                cuts = [t0] + sorted(t for t in edges if t0 < t < t1) + [t1]
                pieces.extend((u0, u1, t0, grouped) for u0, u1 in zip(cuts, cuts[1:]))
            for u0, u1, t0, grouped in pieces:
                first = max(s0 for s0, s1 in spans[i] if s0 <= u0)
                src = raw[i, first][:].rearrange("p (j w) -> p j w", j=PACK)[:, :, u0 - first : u1 - first]
                on_vector = any(s0 <= u0 < s1 for s0, s1 in SHARES[i])
                run = 4 if on_vector else 2
                dst = grouped[:, u0 - t0 : u1 - t0, :].rearrange("p (c i) j -> p c j i", i=run)
                src = src.rearrange("p j (c i) -> p c j i", i=run)
                if on_vector:
                    nc.vector.tensor_copy(out=dst, in_=src)
                else:
                    nc.scalar.activation(dst, src, COPY)

        def quantise(i, t0, t1, grouped):
            first_row = STEPS[i][1]
            plane = lone_plane if i == 0 else shared_planes
            nc.vector.quantize_mx(
                out=words[i][:, t0:t1].bitcast(FP8X4),
                scales=plane[first_row:P, t0:t1],
                in_=grouped[:].rearrange("p w j -> p (w j)"),
            )

        def gather_words(i, s0, s1):
            nc.vector.tensor_copy(slot_words[i][:, s0:s1], words[i][:].bitcast(U32).indirect(entries(offs_t, s0, s1)))

        def multiply(i, e):
            a, first_row = STEPS[i]
            slots = slice(e * C, (e + 1) * C)
            if a < FP8_PASSES:
                g = [a == q and e0 <= e < e1 for q, e0, e1 in W8_LOADS].index(True)
                lhsT = w8[g][:, e - W8_LOADS[g][1], :].bitcast(FP8X4)
                lhsT_scale = w8_planes[W8_ROW:P, 2 * e + a, :]
            else:
                lhsT = w4[a - FP8_PASSES][:, e, :].bitcast(FP4X4)
                lhsT_scale = w4_planes[:, 2 * e + a - FP8_PASSES, :]
            if i == 0:
                g = [e in part for part in LONE_PARTS].index(True)
                first = e - LONE_PARTS[g][0]
                rhs_scale = slot_lone[g][:, first * C : (first + 1) * C]
            else:
                rhs_scale = slot_shared[first_row:P, slots]
            nc.tensor.matmul_mx(
                out=banks[e][:],
                lhsT=lhsT,
                lhsT_scale=lhsT_scale,
                rhs=slot_words[i][:, slots].bitcast(FP8X4),
                rhs_scale=rhs_scale,
                start=(i == 0),
                stop=(i == LAST),
            )

        for i in range(len(STEPS)):
            chunks = [
                (t0, t1, keep.tile([P, t1 - t0, PACK], BF16, name="grouped%d_%d" % (i, t0), align_bytes=64))
                for t0, t1 in QUANTS[i]
            ]
            round_step(i, chunks)
            for t0, t1, grouped in chunks:
                quantise(i, t0, t1, grouped)
            if i == 0:
                gather_words(i, 0, S)
            tag = "slot_lone" if i == 0 else "raw%d_%d" % (i, spans[i][-1][0])
            part = LONE_PARTS[i]
            slot_lone.append(keep.tile([P, len(part) * C], U8, name="slot_lone%d" % i, tag=tag, align_bytes=64))
            nc.vector.tensor_copy(
                slot_lone[i][:], lone_plane[:].indirect(entries(offs_t, C * part[0], C * (part[-1] + 1)))
            )
            if 0 < i < LAST:
                gather_words(i, 0, S)
        nc.scalar.copy(turned_gate[:], gate_bank[:, :BLOCKS])
        for e in range(E):
            multiply(0, e)
        for h in range(2):
            s0, s1 = h * S // 2, (h + 1) * S // 2
            nc.vector.tensor_copy(slot_shared[:, s0:s1], shared_planes[:].indirect(entries(offs_t, s0, s1)))
            for e in range(s0 // C, s1 // C):
                multiply(1, e)
        for e in range(E):
            multiply(2, e)
        for group in GROUPS:
            gather_words(LAST, group[0] * C, (group[-1] + 1) * C)
            for e in group:
                multiply(LAST, e)
                if e != E - 2:
                    nc.scalar.activation(y[:, e * C : (e + 1) * C], banks[e][:], RELU, bias=bias[:, e : e + 1])
                else:
                    nc.vector.tensor_scalar(y[:, e * C : (e + 1) * C], banks[e][:], bias[:, e : e + 1], 0.0, ADD, MAX)

        idle = psum.tile([P, 2 * C], F32, name="idle", tag="spare0")
        nc.tensor.matmul_mx(
            out=idle[:],
            lhsT=w8[-1][:, 0, :].bitcast(FP8X4),
            lhsT_scale=w8_planes[W8_ROW:P, 0, :],
            rhs=slot_words[LAST][:, S - 2 * C :].bitcast(FP8X4),
            rhs_scale=slot_shared[STEPS[LAST][1] : P, S - 2 * C :],
            start=True,
            stop=True,
        )

        def product(r, t0, t1, part):
            j = [r == q and u0 <= t0 < u1 for q, u0, u1 in gate_loads].index(True)
            weights = gates[j][:, t0 - gate_loads[j][1] : t1 - gate_loads[j][1]]
            nc.vector.tensor_tensor(part, y[:].indirect(entries(pos_t[r], t0, t1)), weights, MULT)

        turned = []
        for h, (t0, t1) in enumerate(THIRDS):
            fetched = keep.tile([P, CHUNK], F32, name="fetched%d" % h)
            nc.scalar.activation(fetched[:], y[:].indirect(entries(pos_t[0], t0, t1)), COPY)
            turned.append(psum.tile([P, CHUNK], F32, name="turned%d" % h, tag="bank%d" % h))
            for u in range(0, CHUNK, P):
                nc.tensor.transpose(turned[h][:, u : u + P], fetched[:, u : u + P], ident[:])
        backs = []
        for h, (t0, t1) in enumerate(STORES):
            scaled = keep.tile([P, t1 - t0], F32, name="scaled%d" % h)
            backs.append(psum.tile([P, t1 - t0], F32, name="back%d" % h, tag="bank%d" % (CHUNKS + h) if h < CHUNKS else "spare1"))
            for t in range(t0, t1, P):
                block = slice(t - t0, t - t0 + P)
                source = turned[t // CHUNK][:, t % CHUNK : t % CHUNK + P]
                nc.scalar.activation(scaled[:, block], source, COPY, scale=turned_gate[:, t // P : t // P + 1])
                nc.tensor.transpose(backs[h][:, block], scaled[:, block], ident[:])

        second = keep.tile([P, T], F32, name="second")
        pair = keep.tile([P, T], F32, name="pair")
        for r, t0, t1 in gate_loads[:2]:
            product(r, t0, t1, second[:, t0:t1])
        for stage in range(len(SPANS) + 2):
            if stage < len(SPANS):
                t0, t1 = SPANS[stage]
                product(2, t0, t1, pair[:, t0:t1])
            if 0 <= stage - 2 < len(SPANS):
                t0, t1 = SPANS[stage - 2]
                nc.vector.tensor_tensor(pair[:, t0:t1], pair[:, t0:t1], second[:, t0:t1], ADD)
        for back, (t0, t1) in zip(backs, STORES):
            total = keep.tile([P, t1 - t0], F32, name="total%d" % t0)
            nc.vector.tensor_tensor(total[:], pair[:, t0:t1], back[:], ADD)
            nc.sync.dma_start(out=out[:, t0:t1], in_=total[:])
